import numpy as np
import ml_dtypes


def mxq(x, axis, fmt="e4m3"):
    dtype, down = {"e4m3": (ml_dtypes.float8_e4m3fn, 7), "e5m2": (ml_dtypes.float8_e5m2, 14)}[fmt]
    v = np.moveaxis(np.asarray(x, np.float32).astype(ml_dtypes.bfloat16).astype(np.float64), axis, -1)
    blocks = v.reshape(v.shape[:-1] + (-1, 32))
    amax = np.abs(blocks).max(-1, keepdims=True)
    byte = np.maximum(np.where(amax > 0, np.frexp(amax)[1] - 1 + 127, 0) - down, 1)
    scale = np.exp2(byte - 127.0)
    codes = (blocks / scale).astype(np.float32).astype(dtype).astype(np.float64)
    return np.moveaxis((codes * scale).reshape(v.shape), -1, axis)


WIDE = False


def mx_kscale(k):
    if not WIDE:
        return np.ones(k)
    levels = np.array([10, -10, 5, -5, 0])
    if k % 512:
        return np.exp2(np.random.permutation(np.resize(levels, k // 32))).repeat(32)
    a = np.empty((k // 512, 16))
    for p in range(k // 512):
        a[p, :8] = np.random.permutation(np.resize(levels, 8))
        for g in range(8):
            far = levels[np.abs(levels - a[p, g]) >= 10]
            a[p, g + 8] = far[np.random.randint(len(far))]
    return np.exp2(a.ravel()).repeat(32)


def f64(x):
    return np.asarray(x).astype(np.float64)


def striped(idx):
    return np.tile(idx.reshape(-1, 16).T, (8, 1)).astype(np.uint16)


def unstriped(offs):
    return offs[:16].T.reshape(-1).astype(np.int64)


def pack_weight(w):
    k, n = w.shape
    w = f64(np.asarray(w, np.float32).astype(ml_dtypes.bfloat16)).reshape(k // 32, 32, n)
    amax = np.abs(w).max(1)
    byte = np.clip(np.where(amax > 0, np.frexp(amax)[1] - 1 + 127 - 7, 1), 1, 254)
    scaled = (w * np.exp2(127.0 - byte)[:, None, :]).reshape(k, n).astype(np.float32)
    words = np.ascontiguousarray(scaled.reshape(k // 512, 128, 4, n).transpose(0, 1, 3, 2)).astype(ml_dtypes.float8_e4m3fn).view(np.uint8)
    return words, np.ascontiguousarray(byte.astype(np.uint8).reshape(k // 512, 16, n))


def unpack_weight(words, scales):
    g, p, n, _ = words.shape
    vals = np.ascontiguousarray(words).view(ml_dtypes.float8_e4m3fn).astype(np.float64) * np.repeat(np.exp2(scales.astype(np.float64) - 127.0), 8, axis=1)[..., None]
    return vals.transpose(0, 1, 3, 2).reshape(g * 512, n)


K, T, S, V, N, D = 1024, 2048, 512, 256, 128, 2
P = 2 ** 7


def setup_inputs():
    n = np.random.standard_normal
    s = mx_kscale(K)[:, None]
    packed_xT = pack_weight(n((K, T)) * s)
    return {
        "x_words": packed_xT[0],
        "x_scales": packed_xT[1],
        "w1": (n((K, N)) / np.sqrt(K) / s).astype(np.float32),
        "near": (np.tile(-np.random.uniform(0.0, 1.0, (D, 1, V)), (1, P, 1))).astype(np.float32),
        "sharp": (-np.random.uniform(0.2, 1.0, (N, 1))).astype(np.float32),
        "offs": striped(np.random.permutation(T)[:S]),
        "cen": striped(np.random.permutation(S)[:V]),
        "pos1": striped(np.random.permutation(S)[:V]),
        "pos2": striped(np.random.permutation(S)[:V]),
    }


def reference(x_words, x_scales, w1, near, sharp, offs, cen, pos1, pos2):
    xq = unpack_weight(x_words, x_scales)[:, unstriped(offs)]
    h = mxq(f64(w1), 0, "e4m3").T @ xq
    hc = h[:, unstriped(cen)]
    h0 = h[:, unstriped(pos1)]
    wt0 = np.exp(f64(sharp) * ((h0 - hc) ** 2) + f64(near)[0, :1])
    h1 = h[:, unstriped(pos2)]
    wt1 = np.exp(f64(sharp) * ((h1 - hc) ** 2) + f64(near)[1, :1])
    num = h0 * wt0 + h1 * wt1 + hc
    den = wt0 + wt1 + 1.0
    ss = num / den
    return hc + 1.5 * (hc - ss)

@@ -1,0 +1,140 @@
+from contextlib import ExitStack
+
+import concourse.mybir as mybir
+
+K, T, S, V, N, D = 1024, 2048, 512, 256, 128, 2
+FLOPS = 2 * K * S * N
+
+F32 = mybir.dt.float32
+BF16 = mybir.dt.bfloat16
+I32 = mybir.dt.int32
+U32 = mybir.dt.uint32
+U16 = mybir.dt.uint16
+U8 = mybir.dt.uint8
+FP8X4 = mybir.dt.float8_e4m3fn_x4
+ACT = mybir.ActivationFunctionType
+ALU = mybir.AluOpType
+
+P = 128
+PACK = 4
+PASSES = K // (P * PACK)
+HALF = S // 2
+
+
+def tile_picked_ybilat_sharp_p_kernel(tc, x_words, x_scales, w1, near, sharp, offs, cen, pos1, pos2, out):
+    nc = tc.nc
+    with ExitStack() as ctx:
+        lists = ctx.enter_context(tc.tile_pool(name="lists", bufs=1))
+        sb = ctx.enter_context(tc.tile_pool(name="sb", bufs=1))
+        psum = ctx.enter_context(tc.psum_pool(name="psum", bufs=1))
+
+        offs_t = lists.tile([P, S // 16], U16, name="offs_t")
+        cen_t = lists.tile([P, V // 16], U16, name="cen_t")
+        pos_t = [lists.tile([P, V // 16], U16, name="pos_t%d" % d) for d in range(D)]
+
+        table_scales = sb.tile([P, T], U8, name="table_scales", tag="scales", align_bytes=64)
+        nc.gpsimd.memset(table_scales[:].bitcast(I32), 0)
+        table_words = [sb.tile([P, T], I32, name="table_words%d" % o, tag="table%d" % o, align_bytes=64) for o in range(PASSES)]
+        w_raw = sb.tile([P, PASSES, PACK, N], F32, name="w_raw")
+        near_t = sb.tile([P, D, V], F32, name="near_t")
+        sharp_t = sb.tile([P, 1], F32, name="sharp_t")
+
+        nc.sync.dma_start(offs_t[:], offs)
+        nc.sync.dma_start(out=w_raw[:], in_=w1.rearrange("(o p j) n -> p o j n", o=PASSES, j=PACK))
+        for q in range(4):
+            nc.sync.dma_start(
+                out=table_scales[32 * q : 32 * q + 4 * PASSES, :].bitcast(I32),
+                in_=x_scales[:, 4 * q : 4 * q + 4, :].bitcast(I32),
+            )
+        nc.sync.dma_start(out=table_words[0][:], in_=x_words[0].rearrange("p c r -> p (c r)").bitcast(I32))
+        nc.sync.dma_start(out=table_words[1][:], in_=x_words[1].rearrange("p c r -> p (c r)").bitcast(I32))
+        nc.sync.dma_start(cen_t[:], cen)
+        nc.sync.dma_start(pos_t[0][:], pos1)
+        nc.sync.dma_start(pos_t[1][:], pos2)
+        nc.sync.dma_start(out=near_t[:], in_=near.rearrange("d p v -> p d v"))
+        nc.sync.dma_start(out=sharp_t[:], in_=sharp)
+
+        w_grouped = sb.tile([P, PASSES, N, PACK], BF16, name="w_grouped", tag="grouped", align_bytes=64)
+        nc.scalar.copy(w_grouped[:], w_raw[:].rearrange("p o j n -> p o n j"))
+
+        x_planes = sb.tile([P, S], U8, name="x_planes", align_bytes=64)
+        nc.vector.tensor_copy(x_planes[:], table_scales[:].indirect(offs_t[:]))
+        w_codes = sb.tile([P, PASSES * N], U32, name="w_codes", align_bytes=64)
+        w_scales = sb.tile([P, PASSES * N], U8, name="w_scales", align_bytes=64)
+        nc.vector.quantize_mx(
+            out=w_codes[:].bitcast(FP8X4), scales=w_scales[:], in_=w_grouped[:].rearrange("p o n j -> p (o n j)")
+        )
+
+        x_codes0 = sb.tile([P, S], U32, name="x_codes0", align_bytes=64)
+        nc.vector.tensor_copy(x_codes0[:], table_words[0][:].bitcast(U32).indirect(offs_t[:]))
+
+        groups = [(0, 256), (256, 384), (384, 512)]
+        acc = [psum.tile([N, hi - lo], F32, name="acc%d" % lo) for lo, hi in groups]
+        for bank, (lo, hi) in zip(acc, groups):
+            nc.tensor.matmul_mx(
+                out=bank[:], lhsT=w_codes[:, 0:N].bitcast(FP8X4), lhsT_scale=w_scales[:, 0:N],
+                rhs=x_codes0[:, lo:hi].bitcast(FP8X4), rhs_scale=x_planes[:, lo:hi], start=True, stop=False,
+            )
+        x_codes1 = sb.tile([P, S], U32, name="x_codes1", align_bytes=64)
+        for u in range(2):
+            nc.vector.tensor_copy(
+                x_codes1[:, u * HALF : (u + 1) * HALF],
+                table_words[1][:].bitcast(U32).indirect(offs_t[:, u * HALF // 16 : (u + 1) * HALF // 16]),
+            )
+        h = sb.tile([N, S], F32, name="h")
+        for bank, (lo, hi) in zip(acc, groups):
+            nc.tensor.matmul_mx(
+                out=bank[:], lhsT=w_codes[:, N : 2 * N].bitcast(FP8X4), lhsT_scale=w_scales[:, N : 2 * N],
+                rhs=x_codes1[:, lo:hi].bitcast(FP8X4), rhs_scale=x_planes[4:P, lo:hi], start=False, stop=True,
+            )
+            if hi < S:
+                nc.scalar.copy(h[:, lo:hi], bank[:])
+            else:
+                nc.vector.tensor_copy(h[:, lo:hi], bank[:])
+
+        space = sb.tile([P, D * V], F32, name="space")
+        nc.scalar.activation(space[:], near_t[:].rearrange("p d v -> p (d v)"), ACT.Exp)
+
+        HV = V // 2
+        hc = sb.tile([N, V], F32, name="hc")
+        for lo, hi in [(0, HV), (HV, V)]:
+            nc.vector.tensor_copy(hc[:, lo:hi], h[:].indirect(cen_t[:, lo // 16 : hi // 16]))
+        diff = sb.tile([N, D * V], F32, name="diff")
+        sq = sb.tile([N, D * V], F32, name="sq")
+        rng = sb.tile([N, D * V], F32, name="rng")
+        wt = sb.tile([N, D * V], F32, name="wt")
+        pull = sb.tile([N, D * V], F32, name="pull")
+        far = sb.tile([N, D * V], F32, name="far")
+        first, second = slice(0, V), slice(V, 2 * V)
+        for d, cut in ((0, HV), (1, 192)):
+            for lo, hi in ((0, cut), (cut, V)):
+                at = slice(d * V + lo, d * V + hi)
+                nc.vector.tensor_tensor(diff[:, at], h[:].indirect(pos_t[d][:, lo // 16 : hi // 16]), hc[:, lo:hi], ALU.subtract)
+                nc.scalar.activation(sq[:, at], diff[:, at], ACT.Square)
+            at = slice(d * V, (d + 1) * V)
+            nc.scalar.activation(rng[:, at], sq[:, at], ACT.Exp, scale=sharp_t[:])
+        den = sb.tile([N, V], F32, name="den")
+        den_sq = sb.tile([N, V], F32, name="den_sq")
+        base = sb.tile([N, V], F32, name="base")
+        top = sb.tile([N, V], F32, name="top")
+        nc.vector.tensor_tensor(wt[:, first], rng[:, first], space[:, first], ALU.mult)
+        nc.vector.scalar_tensor_tensor(
+            far[:].rearrange("p (d v) -> p d v", d=D), diff[:].rearrange("p (d v) -> p d v", d=D), -1.5,
+            hc[:].unsqueeze(1).to_broadcast([N, D, V]), ALU.mult, ALU.add,
+        )
+        nc.vector.tensor_tensor(pull[:, first], wt[:, first], far[:, first], ALU.mult)
+        nc.vector.tensor_tensor(wt[:, second], rng[:, second], space[:, second], ALU.mult)
+        nc.vector.tensor_tensor(base[:], pull[:, first], hc[:], ALU.add)
+        nc.vector.scalar_tensor_tensor(den[:], wt[:, first], 1.0, wt[:, second], ALU.add, ALU.add)
+        nc.vector.tensor_tensor(pull[:, second], wt[:, second], far[:, second], ALU.mult)
+        nc.vector.tensor_tensor(den_sq[:], den[:], den[:], ALU.mult)
+        for u in range(2):
+            cols = slice(u * HV, (u + 1) * HV)
+            nc.vector.tensor_tensor(top[:, cols], base[:, cols], pull[:, V + u * HV : V + (u + 1) * HV], ALU.add)
+        for u in range(2):
+            cols = slice(u * HV, (u + 1) * HV)
+            inv = sb.tile([N, HV], F32, name="inv%d" % u)
+            nc.scalar.activation(inv[:], den_sq[:, cols], ACT.Abs_reciprocal_sqrt)
+            res = sb.tile([N, HV], F32, name="res%d" % u)
+            nc.vector.tensor_tensor(res[:], top[:, cols], inv[:], ALU.mult)
+            nc.sync.dma_start(out=out[:, cols], in_=res[:])

@@ -42,7 +42,7 @@ def tile_picked_ybilat_sharp_p_kernel(tc, x_words, x_scales, w1, near, sharp, of
         nc.sync.dma_start(offs_t[:], offs)
         nc.sync.dma_start(out=w_raw[:], in_=w1.rearrange("(o p j) n -> p o j n", o=PASSES, j=PACK))
         for q in range(4):
-            nc.sync.dma_start(
+            nc.gpsimd.dma_start(
                 out=table_scales[32 * q : 32 * q + 4 * PASSES, :].bitcast(I32),
                 in_=x_scales[:, 4 * q : 4 * q + 4, :].bitcast(I32),
             )
@@ -57,8 +57,6 @@ def tile_picked_ybilat_sharp_p_kernel(tc, x_words, x_scales, w1, near, sharp, of
         w_grouped = sb.tile([P, PASSES, N, PACK], BF16, name="w_grouped", tag="grouped", align_bytes=64)
         nc.scalar.copy(w_grouped[:], w_raw[:].rearrange("p o j n -> p o n j"))
 
-        x_planes = sb.tile([P, S], U8, name="x_planes", align_bytes=64)
-        nc.vector.tensor_copy(x_planes[:], table_scales[:].indirect(offs_t[:]))
         w_codes = sb.tile([P, PASSES * N], U32, name="w_codes", align_bytes=64)
         w_scales = sb.tile([P, PASSES * N], U8, name="w_scales", align_bytes=64)
         nc.vector.quantize_mx(
@@ -67,6 +65,8 @@ def tile_picked_ybilat_sharp_p_kernel(tc, x_words, x_scales, w1, near, sharp, of
 
         x_codes0 = sb.tile([P, S], U32, name="x_codes0", align_bytes=64)
         nc.vector.tensor_copy(x_codes0[:], table_words[0][:].bitcast(U32).indirect(offs_t[:]))
+        x_planes = sb.tile([P, S], U8, name="x_planes", tag="table0", align_bytes=64)
+        nc.vector.tensor_copy(x_planes[:], table_scales[:].indirect(offs_t[:]))
 
         groups = [(0, 256), (256, 384), (384, 512)]
         acc = [psum.tile([N, hi - lo], F32, name="acc%d" % lo) for lo, hi in groups]
@@ -75,7 +75,7 @@ def tile_picked_ybilat_sharp_p_kernel(tc, x_words, x_scales, w1, near, sharp, of
                 out=bank[:], lhsT=w_codes[:, 0:N].bitcast(FP8X4), lhsT_scale=w_scales[:, 0:N],
                 rhs=x_codes0[:, lo:hi].bitcast(FP8X4), rhs_scale=x_planes[:, lo:hi], start=True, stop=False,
             )
-        x_codes1 = sb.tile([P, S], U32, name="x_codes1", align_bytes=64)
+        x_codes1 = sb.tile([P, S], U32, name="x_codes1", tag="scales", align_bytes=64)
         for u in range(2):
             nc.vector.tensor_copy(
                 x_codes1[:, u * HALF : (u + 1) * HALF],
@@ -137,4 +137,4 @@ def tile_picked_ybilat_sharp_p_kernel(tc, x_words, x_scales, w1, near, sharp, of
             nc.scalar.activation(inv[:], den_sq[:, cols], ACT.Abs_reciprocal_sqrt)
             res = sb.tile([N, HV], F32, name="res%d" % u)
             nc.vector.tensor_tensor(res[:], top[:, cols], inv[:], ALU.mult)
-            nc.sync.dma_start(out=out[:, cols], in_=res[:])
+            (nc.sync, nc.scalar)[u].dma_start(out=out[:, cols], in_=res[:])

@@ -32,30 +32,32 @@ def tile_picked_ybilat_sharp_p_kernel(tc, x_words, x_scales, w1, near, sharp, of
         cen_t = lists.tile([P, V // 16], U16, name="cen_t")
         pos_t = [lists.tile([P, V // 16], U16, name="pos_t%d" % d) for d in range(D)]
 
-        table_scales = sb.tile([P, T], U8, name="table_scales", tag="scales", align_bytes=64)
-        nc.gpsimd.memset(table_scales[:].bitcast(I32), 0)
+        table_scales = sb.tile([P, T // 4], I32, name="table_scales", tag="scales", align_bytes=64)
+        nc.vector.memset(table_scales[32:64, :], 0)
+        nc.vector.memset(table_scales[64:P, :], 0)
+        x_planes = sb.tile([P, PASSES * S], U8, name="x_planes", align_bytes=64)
+        nc.vector.memset(x_planes[:].bitcast(I32), 0)
         table_words = [sb.tile([P, T], I32, name="table_words%d" % o, tag="table%d" % o, align_bytes=64) for o in range(PASSES)]
-        w_raw = sb.tile([P, PASSES, PACK, N], F32, name="w_raw")
-        near_t = sb.tile([P, D, V], F32, name="near_t")
-        sharp_t = sb.tile([P, 1], F32, name="sharp_t")
+        w_raw = sb.tile([P, PASSES, PACK, N], F32, name="w_raw", tag="raw", align_bytes=64)
 
+        nc.sync.dma_start(out=table_scales[0:32, :], in_=x_scales.rearrange("o q c -> q o c").bitcast(I32))
         nc.sync.dma_start(offs_t[:], offs)
         nc.sync.dma_start(out=w_raw[:], in_=w1.rearrange("(o p j) n -> p o j n", o=PASSES, j=PACK))
-        for q in range(4):
-            nc.gpsimd.dma_start(
-                out=table_scales[32 * q : 32 * q + 4 * PASSES, :].bitcast(I32),
-                in_=x_scales[:, 4 * q : 4 * q + 4, :].bitcast(I32),
-            )
+        nc.sync.dma_start(cen_t[:], cen)
         nc.sync.dma_start(out=table_words[0][:], in_=x_words[0].rearrange("p c r -> p (c r)").bitcast(I32))
         nc.sync.dma_start(out=table_words[1][:], in_=x_words[1].rearrange("p c r -> p (c r)").bitcast(I32))
-        nc.sync.dma_start(cen_t[:], cen)
         nc.sync.dma_start(pos_t[0][:], pos1)
         nc.sync.dma_start(pos_t[1][:], pos2)
-        nc.sync.dma_start(out=near_t[:], in_=near.rearrange("d p v -> p d v"))
-        nc.sync.dma_start(out=sharp_t[:], in_=sharp)
 
+        picked = sb.tile([P, S], U8, name="picked", tag="picked", align_bytes=64)
+        nc.vector.tensor_copy(picked[:], table_scales[:].bitcast(U8).indirect(offs_t[:]))
+        for q in range(4):
+            nc.scalar.dma_start(
+                out=x_planes[32 * q : 32 * q + 4, :].rearrange("r (o c) -> r o c", o=PASSES).bitcast(I32),
+                in_=picked[8 * q : 8 * q + 8, :].bitcast(I32),
+            )
         w_grouped = sb.tile([P, PASSES, N, PACK], BF16, name="w_grouped", tag="grouped", align_bytes=64)
-        nc.scalar.copy(w_grouped[:], w_raw[:].rearrange("p o j n -> p o n j"))
+        nc.vector.tensor_copy(w_grouped[:], w_raw[:].rearrange("p o j n -> p o n j"))
 
         w_codes = sb.tile([P, PASSES * N], U32, name="w_codes", align_bytes=64)
         w_scales = sb.tile([P, PASSES * N], U8, name="w_scales", align_bytes=64)
@@ -65,8 +67,10 @@ def tile_picked_ybilat_sharp_p_kernel(tc, x_words, x_scales, w1, near, sharp, of
 
         x_codes0 = sb.tile([P, S], U32, name="x_codes0", align_bytes=64)
         nc.vector.tensor_copy(x_codes0[:], table_words[0][:].bitcast(U32).indirect(offs_t[:]))
-        x_planes = sb.tile([P, S], U8, name="x_planes", tag="table0", align_bytes=64)
-        nc.vector.tensor_copy(x_planes[:], table_scales[:].indirect(offs_t[:]))
+        near_t = sb.tile([P, D, V], F32, name="near_t", tag="picked", align_bytes=64)
+        sharp_t = sb.tile([P, 1], F32, name="sharp_t", tag="raw", align_bytes=64)
+        nc.sync.dma_start(out=near_t[:], in_=near.rearrange("d p v -> p d v"))
+        nc.sync.dma_start(out=sharp_t[:], in_=sharp)
 
         groups = [(0, 256), (256, 384), (384, 512)]
         acc = [psum.tile([N, hi - lo], F32, name="acc%d" % lo) for lo, hi in groups]
@@ -75,7 +79,7 @@ def tile_picked_ybilat_sharp_p_kernel(tc, x_words, x_scales, w1, near, sharp, of
                 out=bank[:], lhsT=w_codes[:, 0:N].bitcast(FP8X4), lhsT_scale=w_scales[:, 0:N],
                 rhs=x_codes0[:, lo:hi].bitcast(FP8X4), rhs_scale=x_planes[:, lo:hi], start=True, stop=False,
             )
-        x_codes1 = sb.tile([P, S], U32, name="x_codes1", tag="scales", align_bytes=64)
+        x_codes1 = sb.tile([P, S], U32, name="x_codes1", tag="codes1", align_bytes=64)
         for u in range(2):
             nc.vector.tensor_copy(
                 x_codes1[:, u * HALF : (u + 1) * HALF],
@@ -85,14 +89,14 @@ def tile_picked_ybilat_sharp_p_kernel(tc, x_words, x_scales, w1, near, sharp, of
         for bank, (lo, hi) in zip(acc, groups):
             nc.tensor.matmul_mx(
                 out=bank[:], lhsT=w_codes[:, N : 2 * N].bitcast(FP8X4), lhsT_scale=w_scales[:, N : 2 * N],
-                rhs=x_codes1[:, lo:hi].bitcast(FP8X4), rhs_scale=x_planes[4:P, lo:hi], start=False, stop=True,
+                rhs=x_codes1[:, lo:hi].bitcast(FP8X4), rhs_scale=x_planes[:, S + lo : S + hi], start=False, stop=True,
             )
-            if hi < S:
+            if lo != HALF:
                 nc.scalar.copy(h[:, lo:hi], bank[:])
             else:
                 nc.vector.tensor_copy(h[:, lo:hi], bank[:])
 
-        space = sb.tile([P, D * V], F32, name="space")
+        space = sb.tile([P, D * V], F32, name="space", tag="codes1", align_bytes=64)
         nc.scalar.activation(space[:], near_t[:].rearrange("p d v -> p (d v)"), ACT.Exp)
 
         HV = V // 2
@@ -106,35 +110,41 @@ def tile_picked_ybilat_sharp_p_kernel(tc, x_words, x_scales, w1, near, sharp, of
         pull = sb.tile([N, D * V], F32, name="pull")
         far = sb.tile([N, D * V], F32, name="far")
         first, second = slice(0, V), slice(V, 2 * V)
-        for d, cut in ((0, HV), (1, 192)):
+        LAST = 64
+        body, last = slice(V, 2 * V - LAST), slice(2 * V - LAST, 2 * V)
+        for d, cut in ((0, HV), (1, V - LAST)):
             for lo, hi in ((0, cut), (cut, V)):
                 at = slice(d * V + lo, d * V + hi)
                 nc.vector.tensor_tensor(diff[:, at], h[:].indirect(pos_t[d][:, lo // 16 : hi // 16]), hc[:, lo:hi], ALU.subtract)
-                nc.scalar.activation(sq[:, at], diff[:, at], ACT.Square)
-            at = slice(d * V, (d + 1) * V)
+                if at != last:
+                    nc.scalar.activation(sq[:, at], diff[:, at], ACT.Square)
+            at = (first, body)[d]
             nc.scalar.activation(rng[:, at], sq[:, at], ACT.Exp, scale=sharp_t[:])
         den = sb.tile([N, V], F32, name="den")
         den_sq = sb.tile([N, V], F32, name="den_sq")
         base = sb.tile([N, V], F32, name="base")
         top = sb.tile([N, V], F32, name="top")
+        nc.vector.scalar_tensor_tensor(far[:, first], diff[:, first], -1.5, hc[:], ALU.mult, ALU.add)
+        nc.vector.tensor_tensor(sq[:, last], diff[:, last], diff[:, last], ALU.mult)
+        nc.scalar.activation(rng[:, last], sq[:, last], ACT.Exp, scale=sharp_t[:])
         nc.vector.tensor_tensor(wt[:, first], rng[:, first], space[:, first], ALU.mult)
-        nc.vector.scalar_tensor_tensor(
-            far[:].rearrange("p (d v) -> p d v", d=D), diff[:].rearrange("p (d v) -> p d v", d=D), -1.5,
-            hc[:].unsqueeze(1).to_broadcast([N, D, V]), ALU.mult, ALU.add,
-        )
-        nc.vector.tensor_tensor(pull[:, first], wt[:, first], far[:, first], ALU.mult)
+        nc.vector.scalar_tensor_tensor(far[:, second], diff[:, second], -1.5, hc[:], ALU.mult, ALU.add)
         nc.vector.tensor_tensor(wt[:, second], rng[:, second], space[:, second], ALU.mult)
-        nc.vector.tensor_tensor(base[:], pull[:, first], hc[:], ALU.add)
+        nc.vector.tensor_tensor(sq[:, second], wt[:, first], far[:, first], ALU.mult)
         nc.vector.scalar_tensor_tensor(den[:], wt[:, first], 1.0, wt[:, second], ALU.add, ALU.add)
-        nc.vector.tensor_tensor(pull[:, second], wt[:, second], far[:, second], ALU.mult)
-        nc.vector.tensor_tensor(den_sq[:], den[:], den[:], ALU.mult)
+        nc.vector.tensor_tensor(base[:], sq[:, second], hc[:], ALU.add)
+        nc.vector.tensor_tensor(den_sq[:, 0:HV], den[:, 0:HV], den[:, 0:HV], ALU.mult)
+        nc.scalar.activation(den_sq[:, HV:V], den[:, HV:V], ACT.Abs_reciprocal_sqrt)
+        for u in range(2):
+            at = slice(V + u * HV, V + (u + 1) * HV)
+            nc.vector.tensor_tensor(pull[:, at], wt[:, at], far[:, at], ALU.mult)
         for u in range(2):
             cols = slice(u * HV, (u + 1) * HV)
             nc.vector.tensor_tensor(top[:, cols], base[:, cols], pull[:, V + u * HV : V + (u + 1) * HV], ALU.add)
         for u in range(2):
             cols = slice(u * HV, (u + 1) * HV)
             inv = sb.tile([N, HV], F32, name="inv%d" % u)
-            nc.scalar.activation(inv[:], den_sq[:, cols], ACT.Abs_reciprocal_sqrt)
+            nc.scalar.activation(inv[:], den_sq[:, cols], (ACT.Abs_reciprocal_sqrt, ACT.Square)[u])
             res = sb.tile([N, HV], F32, name="res%d" % u)
             nc.vector.tensor_tensor(res[:], top[:, cols], inv[:], ALU.mult)
             (nc.sync, nc.scalar)[u].dma_start(out=out[:, cols], in_=res[:])

@@ -18,7 +18,15 @@ ALU = mybir.AluOpType
 P = 128
 PACK = 4
 PASSES = K // (P * PACK)
-HALF = S // 2
+QUADS = 4
+QUAD_ROWS = 4
+SCALE_ROWS = PASSES * QUADS * QUAD_ROWS
+PER_COL = 16
+HALF_S = S // 2
+HALF_V = V // 2
+SHARPEN = 1.5
+BANK_COLS = ((0, HALF_S), (HALF_S, HALF_S + HALF_S // 2), (HALF_S + HALF_S // 2, S))
+LAST = 64
 
 
 def tile_picked_ybilat_sharp_p_kernel(tc, x_words, x_scales, w1, near, sharp, offs, cen, pos1, pos2, out):
@@ -28,19 +36,19 @@ def tile_picked_ybilat_sharp_p_kernel(tc, x_words, x_scales, w1, near, sharp, of
         sb = ctx.enter_context(tc.tile_pool(name="sb", bufs=1))
         psum = ctx.enter_context(tc.psum_pool(name="psum", bufs=1))
 
-        offs_t = lists.tile([P, S // 16], U16, name="offs_t")
-        cen_t = lists.tile([P, V // 16], U16, name="cen_t")
-        pos_t = [lists.tile([P, V // 16], U16, name="pos_t%d" % d) for d in range(D)]
+        offs_t = lists.tile([P, S // PER_COL], U16, name="offs_t")
+        cen_t = lists.tile([P, V // PER_COL], U16, name="cen_t")
+        pos_t = [lists.tile([P, V // PER_COL], U16, name="pos_t%d" % d) for d in range(D)]
 
-        table_scales = sb.tile([P, T // 4], I32, name="table_scales", tag="scales", align_bytes=64)
-        nc.vector.memset(table_scales[32:64, :], 0)
-        nc.vector.memset(table_scales[64:P, :], 0)
+        table_scales = sb.tile([P, T // 4], I32, name="table_scales", align_bytes=64)
+        nc.vector.memset(table_scales[SCALE_ROWS : P // 2, :], 0)
+        nc.vector.memset(table_scales[P // 2 : P, :], 0)
         x_planes = sb.tile([P, PASSES * S], U8, name="x_planes", align_bytes=64)
         nc.vector.memset(x_planes[:].bitcast(I32), 0)
-        table_words = [sb.tile([P, T], I32, name="table_words%d" % o, tag="table%d" % o, align_bytes=64) for o in range(PASSES)]
-        w_raw = sb.tile([P, PASSES, PACK, N], F32, name="w_raw", tag="raw", align_bytes=64)
+        table_words = [sb.tile([P, T], I32, name="table_words%d" % o, align_bytes=64) for o in range(PASSES)]
+        w_raw = sb.tile([P, PASSES, PACK, N], F32, name="w_raw", tag="w_raw_then_sharp", align_bytes=64)
 
-        nc.sync.dma_start(out=table_scales[0:32, :], in_=x_scales.rearrange("o q c -> q o c").bitcast(I32))
+        nc.sync.dma_start(out=table_scales[0:SCALE_ROWS, :], in_=x_scales.rearrange("o q c -> q o c").bitcast(I32))
         nc.sync.dma_start(offs_t[:], offs)
         nc.sync.dma_start(out=w_raw[:], in_=w1.rearrange("(o p j) n -> p o j n", o=PASSES, j=PACK))
         nc.sync.dma_start(cen_t[:], cen)
@@ -49,16 +57,17 @@ def tile_picked_ybilat_sharp_p_kernel(tc, x_words, x_scales, w1, near, sharp, of
         nc.sync.dma_start(pos_t[0][:], pos1)
         nc.sync.dma_start(pos_t[1][:], pos2)
 
-        picked = sb.tile([P, S], U8, name="picked", tag="picked", align_bytes=64)
+        picked = sb.tile([P, S], U8, name="picked", tag="picked_then_near", align_bytes=64)
         nc.vector.tensor_copy(picked[:], table_scales[:].bitcast(U8).indirect(offs_t[:]))
-        for q in range(4):
+        rows = PASSES * QUAD_ROWS
+        for q in range(QUADS):
             nc.scalar.dma_start(
-                out=x_planes[32 * q : 32 * q + 4, :].rearrange("r (o c) -> r o c", o=PASSES).bitcast(I32),
-                in_=picked[8 * q : 8 * q + 8, :].bitcast(I32),
+                out=x_planes[32 * q : 32 * q + QUAD_ROWS, :].rearrange("r (o c) -> r o c", o=PASSES).bitcast(I32),
+                in_=picked[rows * q : rows * (q + 1), :].bitcast(I32),
             )
-        w_grouped = sb.tile([P, PASSES, N, PACK], BF16, name="w_grouped", tag="grouped", align_bytes=64)
-        nc.vector.tensor_copy(w_grouped[:], w_raw[:].rearrange("p o j n -> p o n j"))
 
+        w_grouped = sb.tile([P, PASSES, N, PACK], BF16, name="w_grouped", align_bytes=64)
+        nc.vector.tensor_copy(w_grouped[:], w_raw[:].rearrange("p o j n -> p o n j"))
         w_codes = sb.tile([P, PASSES * N], U32, name="w_codes", align_bytes=64)
         w_scales = sb.tile([P, PASSES * N], U8, name="w_scales", align_bytes=64)
         nc.vector.quantize_mx(
@@ -67,84 +76,89 @@ def tile_picked_ybilat_sharp_p_kernel(tc, x_words, x_scales, w1, near, sharp, of
 
         x_codes0 = sb.tile([P, S], U32, name="x_codes0", align_bytes=64)
         nc.vector.tensor_copy(x_codes0[:], table_words[0][:].bitcast(U32).indirect(offs_t[:]))
-        near_t = sb.tile([P, D, V], F32, name="near_t", tag="picked", align_bytes=64)
-        sharp_t = sb.tile([P, 1], F32, name="sharp_t", tag="raw", align_bytes=64)
+
+        near_t = sb.tile([P, D, V], F32, name="near_t", tag="picked_then_near", align_bytes=64)
+        sharp_t = sb.tile([P, 1], F32, name="sharp_t", tag="w_raw_then_sharp", align_bytes=64)
         nc.sync.dma_start(out=near_t[:], in_=near.rearrange("d p v -> p d v"))
         nc.sync.dma_start(out=sharp_t[:], in_=sharp)
 
-        groups = [(0, 256), (256, 384), (384, 512)]
-        acc = [psum.tile([N, hi - lo], F32, name="acc%d" % lo) for lo, hi in groups]
-        for bank, (lo, hi) in zip(acc, groups):
+        banks = [psum.tile([N, hi - lo], F32, name="bank%d" % lo) for lo, hi in BANK_COLS]
+        for bank, (lo, hi) in zip(banks, BANK_COLS):
             nc.tensor.matmul_mx(
                 out=bank[:], lhsT=w_codes[:, 0:N].bitcast(FP8X4), lhsT_scale=w_scales[:, 0:N],
                 rhs=x_codes0[:, lo:hi].bitcast(FP8X4), rhs_scale=x_planes[:, lo:hi], start=True, stop=False,
             )
-        x_codes1 = sb.tile([P, S], U32, name="x_codes1", tag="codes1", align_bytes=64)
-        for u in range(2):
+        x_codes1 = sb.tile([P, S], U32, name="x_codes1", tag="codes1_then_space", align_bytes=64)
+        for lo, hi in ((0, HALF_S), (HALF_S, S)):
             nc.vector.tensor_copy(
-                x_codes1[:, u * HALF : (u + 1) * HALF],
-                table_words[1][:].bitcast(U32).indirect(offs_t[:, u * HALF // 16 : (u + 1) * HALF // 16]),
+                x_codes1[:, lo:hi],
+                table_words[1][:].bitcast(U32).indirect(offs_t[:, lo // PER_COL : hi // PER_COL]),
             )
         h = sb.tile([N, S], F32, name="h")
-        for bank, (lo, hi) in zip(acc, groups):
+        copies_out = (nc.scalar.copy, nc.vector.tensor_copy, nc.scalar.copy)
+        for bank, (lo, hi), copy_out in zip(banks, BANK_COLS, copies_out):
             nc.tensor.matmul_mx(
                 out=bank[:], lhsT=w_codes[:, N : 2 * N].bitcast(FP8X4), lhsT_scale=w_scales[:, N : 2 * N],
                 rhs=x_codes1[:, lo:hi].bitcast(FP8X4), rhs_scale=x_planes[:, S + lo : S + hi], start=False, stop=True,
             )
-            if lo != HALF:
-                nc.scalar.copy(h[:, lo:hi], bank[:])
-            else:
-                nc.vector.tensor_copy(h[:, lo:hi], bank[:])
+            copy_out(h[:, lo:hi], bank[:])
 
-        space = sb.tile([P, D * V], F32, name="space", tag="codes1", align_bytes=64)
+        space = sb.tile([P, D * V], F32, name="space", tag="codes1_then_space", align_bytes=64)
         nc.scalar.activation(space[:], near_t[:].rearrange("p d v -> p (d v)"), ACT.Exp)
 
-        HV = V // 2
         hc = sb.tile([N, V], F32, name="hc")
-        for lo, hi in [(0, HV), (HV, V)]:
-            nc.vector.tensor_copy(hc[:, lo:hi], h[:].indirect(cen_t[:, lo // 16 : hi // 16]))
+        for lo, hi in ((0, HALF_V), (HALF_V, V)):
+            nc.vector.tensor_copy(hc[:, lo:hi], h[:].indirect(cen_t[:, lo // PER_COL : hi // PER_COL]))
+
         diff = sb.tile([N, D * V], F32, name="diff")
-        sq = sb.tile([N, D * V], F32, name="sq")
-        rng = sb.tile([N, D * V], F32, name="rng")
+        diff_sq = sb.tile([N, D * V], F32, name="diff_sq")
+        alike = sb.tile([N, D * V], F32, name="alike")
         wt = sb.tile([N, D * V], F32, name="wt")
-        pull = sb.tile([N, D * V], F32, name="pull")
         far = sb.tile([N, D * V], F32, name="far")
         first, second = slice(0, V), slice(V, 2 * V)
-        LAST = 64
         body, last = slice(V, 2 * V - LAST), slice(2 * V - LAST, 2 * V)
-        for d, cut in ((0, HV), (1, V - LAST)):
+        for d, cut, exp_cols in ((0, HALF_V, first), (1, V - LAST, body)):
             for lo, hi in ((0, cut), (cut, V)):
                 at = slice(d * V + lo, d * V + hi)
-                nc.vector.tensor_tensor(diff[:, at], h[:].indirect(pos_t[d][:, lo // 16 : hi // 16]), hc[:, lo:hi], ALU.subtract)
+                looked_up = h[:].indirect(pos_t[d][:, lo // PER_COL : hi // PER_COL])
+                nc.vector.tensor_tensor(diff[:, at], looked_up, hc[:, lo:hi], ALU.subtract)
                 if at != last:
-                    nc.scalar.activation(sq[:, at], diff[:, at], ACT.Square)
-            at = (first, body)[d]
-            nc.scalar.activation(rng[:, at], sq[:, at], ACT.Exp, scale=sharp_t[:])
+                    nc.scalar.activation(diff_sq[:, at], diff[:, at], ACT.Square)
+            nc.scalar.activation(alike[:, exp_cols], diff_sq[:, exp_cols], ACT.Exp, scale=sharp_t[:])
+
         den = sb.tile([N, V], F32, name="den")
-        den_sq = sb.tile([N, V], F32, name="den_sq")
+        den_sq = sb.tile([N, HALF_V], F32, name="den_sq")
+        den_rsqrt = sb.tile([N, HALF_V], F32, name="den_rsqrt")
         base = sb.tile([N, V], F32, name="base")
+        pull1 = sb.tile([N, V], F32, name="pull1")
         top = sb.tile([N, V], F32, name="top")
-        nc.vector.scalar_tensor_tensor(far[:, first], diff[:, first], -1.5, hc[:], ALU.mult, ALU.add)
-        nc.vector.tensor_tensor(sq[:, last], diff[:, last], diff[:, last], ALU.mult)
-        nc.scalar.activation(rng[:, last], sq[:, last], ACT.Exp, scale=sharp_t[:])
-        nc.vector.tensor_tensor(wt[:, first], rng[:, first], space[:, first], ALU.mult)
-        nc.vector.scalar_tensor_tensor(far[:, second], diff[:, second], -1.5, hc[:], ALU.mult, ALU.add)
-        nc.vector.tensor_tensor(wt[:, second], rng[:, second], space[:, second], ALU.mult)
-        nc.vector.tensor_tensor(sq[:, second], wt[:, first], far[:, first], ALU.mult)
+        pull0 = diff_sq[:, second]
+        left, right = slice(0, HALF_V), slice(HALF_V, V)
+
+        nc.vector.scalar_tensor_tensor(far[:, first], diff[:, first], -SHARPEN, hc[:], ALU.mult, ALU.add)
+        nc.vector.tensor_tensor(diff_sq[:, last], diff[:, last], diff[:, last], ALU.mult)
+        nc.scalar.activation(alike[:, last], diff_sq[:, last], ACT.Exp, scale=sharp_t[:])
+        nc.vector.tensor_tensor(wt[:, first], alike[:, first], space[:, first], ALU.mult)
+        nc.vector.scalar_tensor_tensor(far[:, second], diff[:, second], -SHARPEN, hc[:], ALU.mult, ALU.add)
+        nc.vector.tensor_tensor(wt[:, second], alike[:, second], space[:, second], ALU.mult)
+        nc.vector.tensor_tensor(pull0, wt[:, first], far[:, first], ALU.mult)
         nc.vector.scalar_tensor_tensor(den[:], wt[:, first], 1.0, wt[:, second], ALU.add, ALU.add)
-        nc.vector.tensor_tensor(base[:], sq[:, second], hc[:], ALU.add)
-        nc.vector.tensor_tensor(den_sq[:, 0:HV], den[:, 0:HV], den[:, 0:HV], ALU.mult)
-        nc.scalar.activation(den_sq[:, HV:V], den[:, HV:V], ACT.Abs_reciprocal_sqrt)
-        for u in range(2):
-            at = slice(V + u * HV, V + (u + 1) * HV)
-            nc.vector.tensor_tensor(pull[:, at], wt[:, at], far[:, at], ALU.mult)
-        for u in range(2):
-            cols = slice(u * HV, (u + 1) * HV)
-            nc.vector.tensor_tensor(top[:, cols], base[:, cols], pull[:, V + u * HV : V + (u + 1) * HV], ALU.add)
-        for u in range(2):
-            cols = slice(u * HV, (u + 1) * HV)
-            inv = sb.tile([N, HV], F32, name="inv%d" % u)
-            nc.scalar.activation(inv[:], den_sq[:, cols], (ACT.Abs_reciprocal_sqrt, ACT.Square)[u])
-            res = sb.tile([N, HV], F32, name="res%d" % u)
-            nc.vector.tensor_tensor(res[:], top[:, cols], inv[:], ALU.mult)
-            (nc.sync, nc.scalar)[u].dma_start(out=out[:, cols], in_=res[:])
+        nc.vector.tensor_tensor(base[:], pull0, hc[:], ALU.add)
+
+        nc.vector.tensor_tensor(den_sq[:], den[:, left], den[:, left], ALU.mult)
+        nc.scalar.activation(den_rsqrt[:], den[:, right], ACT.Abs_reciprocal_sqrt)
+        for cols in (left, right):
+            at = slice(V + cols.start, V + cols.stop)
+            nc.vector.tensor_tensor(pull1[:, cols], wt[:, at], far[:, at], ALU.mult)
+        for cols in (left, right):
+            nc.vector.tensor_tensor(top[:, cols], base[:, cols], pull1[:, cols], ALU.add)
+        halves = (
+            (left, den_sq, ACT.Abs_reciprocal_sqrt, nc.sync),
+            (right, den_rsqrt, ACT.Square, nc.scalar),
+        )
+        for cols, source, func, queue in halves:
+            inv_den = sb.tile([N, HALF_V], F32, name="inv_den%d" % cols.start)
+            nc.scalar.activation(inv_den[:], source[:], func)
+            result = sb.tile([N, HALF_V], F32, name="result%d" % cols.start)
+            nc.vector.tensor_tensor(result[:], top[:, cols], inv_den[:], ALU.mult)
+            queue.dma_start(out=out[:, cols], in_=result[:])

@@ -21,6 +21,7 @@ PASSES = K // (P * PACK)
 QUADS = 4
 QUAD_ROWS = 4
 SCALE_ROWS = PASSES * QUADS * QUAD_ROWS
+ROW_STEP = P // SCALE_ROWS
 PER_COL = 16
 HALF_S = S // 2
 HALF_V = V // 2
@@ -40,30 +41,28 @@ def tile_picked_ybilat_sharp_p_kernel(tc, x_words, x_scales, w1, near, sharp, of
         cen_t = lists.tile([P, V // PER_COL], U16, name="cen_t")
         pos_t = [lists.tile([P, V // PER_COL], U16, name="pos_t%d" % d) for d in range(D)]
 
-        table_scales = sb.tile([P, T // 4], I32, name="table_scales", align_bytes=64)
-        nc.vector.memset(table_scales[SCALE_ROWS : P // 2, :], 0)
-        nc.vector.memset(table_scales[P // 2 : P, :], 0)
+        table_scales = sb.tile([P, T // 4], I32, name="table_scales", tag="scales_then_near", align_bytes=64)
+        nc.vector.memset(table_scales[:], 0)
         x_planes = sb.tile([P, PASSES * S], U8, name="x_planes", align_bytes=64)
         nc.vector.memset(x_planes[:].bitcast(I32), 0)
         table_words = [sb.tile([P, T], I32, name="table_words%d" % o, align_bytes=64) for o in range(PASSES)]
-        w_raw = sb.tile([P, PASSES, PACK, N], F32, name="w_raw", tag="w_raw_then_sharp", align_bytes=64)
+        w_raw = sb.tile([P, PASSES, PACK, N], F32, name="w_raw", align_bytes=64)
 
-        nc.sync.dma_start(out=table_scales[0:SCALE_ROWS, :], in_=x_scales.rearrange("o q c -> q o c").bitcast(I32))
-        nc.sync.dma_start(offs_t[:], offs)
         nc.sync.dma_start(out=w_raw[:], in_=w1.rearrange("(o p j) n -> p o j n", o=PASSES, j=PACK))
-        nc.sync.dma_start(cen_t[:], cen)
+        nc.sync.dma_start(out=table_scales[0:P:ROW_STEP, :], in_=x_scales.rearrange("o q c -> q o c").bitcast(I32))
+        nc.sync.dma_start(offs_t[:], offs)
         nc.sync.dma_start(out=table_words[0][:], in_=x_words[0].rearrange("p c r -> p (c r)").bitcast(I32))
         nc.sync.dma_start(out=table_words[1][:], in_=x_words[1].rearrange("p c r -> p (c r)").bitcast(I32))
+        nc.sync.dma_start(cen_t[:], cen)
         nc.sync.dma_start(pos_t[0][:], pos1)
         nc.sync.dma_start(pos_t[1][:], pos2)
 
-        picked = sb.tile([P, S], U8, name="picked", tag="picked_then_near", align_bytes=64)
+        picked = sb.tile([P, S], U8, name="picked", align_bytes=64)
         nc.vector.tensor_copy(picked[:], table_scales[:].bitcast(U8).indirect(offs_t[:]))
-        rows = PASSES * QUAD_ROWS
         for q in range(QUADS):
-            nc.scalar.dma_start(
+            nc.sync.dma_start(
                 out=x_planes[32 * q : 32 * q + QUAD_ROWS, :].rearrange("r (o c) -> r o c", o=PASSES).bitcast(I32),
-                in_=picked[rows * q : rows * (q + 1), :].bitcast(I32),
+                in_=picked[32 * q : 32 * (q + 1) : ROW_STEP, :].bitcast(I32),
             )
 
         w_grouped = sb.tile([P, PASSES, N, PACK], BF16, name="w_grouped", align_bytes=64)
@@ -77,10 +76,11 @@ def tile_picked_ybilat_sharp_p_kernel(tc, x_words, x_scales, w1, near, sharp, of
         x_codes0 = sb.tile([P, S], U32, name="x_codes0", align_bytes=64)
         nc.vector.tensor_copy(x_codes0[:], table_words[0][:].bitcast(U32).indirect(offs_t[:]))
 
-        near_t = sb.tile([P, D, V], F32, name="near_t", tag="picked_then_near", align_bytes=64)
-        sharp_t = sb.tile([P, 1], F32, name="sharp_t", tag="w_raw_then_sharp", align_bytes=64)
-        nc.sync.dma_start(out=near_t[:], in_=near.rearrange("d p v -> p d v"))
-        nc.sync.dma_start(out=sharp_t[:], in_=sharp)
+        near_sharp = sb.tile([P, D * V + 1], F32, name="near_sharp", tag="scales_then_near", align_bytes=64)
+        near_t = near_sharp[:, 0 : D * V]
+        sharp_t = near_sharp[:, D * V : D * V + 1]
+        nc.sync.dma_start(out=near_t.rearrange("p (d v) -> p d v", d=D), in_=near.rearrange("d p v -> p d v"))
+        nc.sync.dma_start(out=sharp_t, in_=sharp)
 
         banks = [psum.tile([N, hi - lo], F32, name="bank%d" % lo) for lo, hi in BANK_COLS]
         for bank, (lo, hi) in zip(banks, BANK_COLS):
@@ -104,7 +104,7 @@ def tile_picked_ybilat_sharp_p_kernel(tc, x_words, x_scales, w1, near, sharp, of
             copy_out(h[:, lo:hi], bank[:])
 
         space = sb.tile([P, D * V], F32, name="space", tag="codes1_then_space", align_bytes=64)
-        nc.scalar.activation(space[:], near_t[:].rearrange("p d v -> p (d v)"), ACT.Exp)
+        nc.scalar.activation(space[:], near_t, ACT.Exp)
 
         hc = sb.tile([N, V], F32, name="hc")
         for lo, hi in ((0, HALF_V), (HALF_V, V)):
@@ -124,7 +124,7 @@ def tile_picked_ybilat_sharp_p_kernel(tc, x_words, x_scales, w1, near, sharp, of
                 nc.vector.tensor_tensor(diff[:, at], looked_up, hc[:, lo:hi], ALU.subtract)
                 if at != last:
                     nc.scalar.activation(diff_sq[:, at], diff[:, at], ACT.Square)
-            nc.scalar.activation(alike[:, exp_cols], diff_sq[:, exp_cols], ACT.Exp, scale=sharp_t[:])
+            nc.scalar.activation(alike[:, exp_cols], diff_sq[:, exp_cols], ACT.Exp, scale=sharp_t)
 
         den = sb.tile([N, V], F32, name="den")
         den_sq = sb.tile([N, HALF_V], F32, name="den_sq")
@@ -137,7 +137,7 @@ def tile_picked_ybilat_sharp_p_kernel(tc, x_words, x_scales, w1, near, sharp, of
 
         nc.vector.scalar_tensor_tensor(far[:, first], diff[:, first], -SHARPEN, hc[:], ALU.mult, ALU.add)
         nc.vector.tensor_tensor(diff_sq[:, last], diff[:, last], diff[:, last], ALU.mult)
-        nc.scalar.activation(alike[:, last], diff_sq[:, last], ACT.Exp, scale=sharp_t[:])
+        nc.scalar.activation(alike[:, last], diff_sq[:, last], ACT.Exp, scale=sharp_t)
         nc.vector.tensor_tensor(wt[:, first], alike[:, first], space[:, first], ALU.mult)
         nc.vector.scalar_tensor_tensor(far[:, second], diff[:, second], -SHARPEN, hc[:], ALU.mult, ALU.add)
         nc.vector.tensor_tensor(wt[:, second], alike[:, second], space[:, second], ALU.mult)

@@ -41,7 +41,7 @@ def tile_picked_ybilat_sharp_p_kernel(tc, x_words, x_scales, w1, near, sharp, of
         cen_t = lists.tile([P, V // PER_COL], U16, name="cen_t")
         pos_t = [lists.tile([P, V // PER_COL], U16, name="pos_t%d" % d) for d in range(D)]
 
-        table_scales = sb.tile([P, T // 4], I32, name="table_scales", tag="scales_then_near", align_bytes=64)
+        table_scales = sb.tile([P, T // 4], I32, name="table_scales", align_bytes=64)
         nc.vector.memset(table_scales[:], 0)
         x_planes = sb.tile([P, PASSES * S], U8, name="x_planes", align_bytes=64)
         nc.vector.memset(x_planes[:].bitcast(I32), 0)
@@ -57,10 +57,10 @@ def tile_picked_ybilat_sharp_p_kernel(tc, x_words, x_scales, w1, near, sharp, of
         nc.sync.dma_start(pos_t[0][:], pos1)
         nc.sync.dma_start(pos_t[1][:], pos2)
 
-        picked = sb.tile([P, S], U8, name="picked", align_bytes=64)
+        picked = sb.tile([P, S], U8, name="picked", tag="picked_then_near", align_bytes=64)
         nc.vector.tensor_copy(picked[:], table_scales[:].bitcast(U8).indirect(offs_t[:]))
         for q in range(QUADS):
-            nc.sync.dma_start(
+            nc.scalar.dma_start(
                 out=x_planes[32 * q : 32 * q + QUAD_ROWS, :].rearrange("r (o c) -> r o c", o=PASSES).bitcast(I32),
                 in_=picked[32 * q : 32 * (q + 1) : ROW_STEP, :].bitcast(I32),
             )
@@ -76,7 +76,7 @@ def tile_picked_ybilat_sharp_p_kernel(tc, x_words, x_scales, w1, near, sharp, of
         x_codes0 = sb.tile([P, S], U32, name="x_codes0", align_bytes=64)
         nc.vector.tensor_copy(x_codes0[:], table_words[0][:].bitcast(U32).indirect(offs_t[:]))
 
-        near_sharp = sb.tile([P, D * V + 1], F32, name="near_sharp", tag="scales_then_near", align_bytes=64)
+        near_sharp = sb.tile([P, D * V + 1], F32, name="near_sharp", tag="picked_then_near", align_bytes=64)
         near_t = near_sharp[:, 0 : D * V]
         sharp_t = near_sharp[:, D * V : D * V + 1]
         nc.sync.dma_start(out=near_t.rearrange("p (d v) -> p d v", d=D), in_=near.rearrange("d p v -> p d v"))

@@ -1,6 +1,7 @@
 from contextlib import ExitStack
 
 import concourse.mybir as mybir
+from concourse.masks import make_identity
 
 K, T, S, V, N, D = 1024, 2048, 512, 256, 128, 2
 FLOPS = 2 * K * S * N
@@ -45,12 +46,17 @@ def tile_picked_ybilat_sharp_p_kernel(tc, x_words, x_scales, w1, near, sharp, of
         nc.vector.memset(table_scales[:], 0)
         x_planes = sb.tile([P, PASSES * S], U8, name="x_planes", align_bytes=64)
         nc.vector.memset(x_planes[:].bitcast(I32), 0)
+        near_rows = sb.tile([P, V], F32, name="near_rows")
+        nc.gpsimd.memset(near_rows[:], 0.0)
+        identity = sb.tile([P, P], F32, name="identity")
+        make_identity(nc, identity[:])
         table_words = [sb.tile([P, T], I32, name="table_words%d" % o, align_bytes=64) for o in range(PASSES)]
         w_raw = sb.tile([P, PASSES, PACK, N], F32, name="w_raw", align_bytes=64)
 
         nc.sync.dma_start(out=w_raw[:], in_=w1.rearrange("(o p j) n -> p o j n", o=PASSES, j=PACK))
         nc.sync.dma_start(out=table_scales[0:P:ROW_STEP, :], in_=x_scales.rearrange("o q c -> q o c").bitcast(I32))
         nc.sync.dma_start(offs_t[:], offs)
+        nc.sync.dma_start(out=near_rows[0:D, :], in_=near[:, 0, :])
         nc.sync.dma_start(out=table_words[0][:], in_=x_words[0].rearrange("p c r -> p (c r)").bitcast(I32))
         nc.sync.dma_start(out=table_words[1][:], in_=x_words[1].rearrange("p c r -> p (c r)").bitcast(I32))
         nc.sync.dma_start(cen_t[:], cen)
@@ -66,7 +72,7 @@ def tile_picked_ybilat_sharp_p_kernel(tc, x_words, x_scales, w1, near, sharp, of
             )
 
         w_grouped = sb.tile([P, PASSES, N, PACK], BF16, name="w_grouped", align_bytes=64)
-        nc.vector.tensor_copy(w_grouped[:], w_raw[:].rearrange("p o j n -> p o n j"))
+        nc.scalar.copy(w_grouped[:], w_raw[:].rearrange("p o j n -> p o n j"))
         w_codes = sb.tile([P, PASSES * N], U32, name="w_codes", align_bytes=64)
         w_scales = sb.tile([P, PASSES * N], U8, name="w_scales", align_bytes=64)
         nc.vector.quantize_mx(
@@ -76,11 +82,23 @@ def tile_picked_ybilat_sharp_p_kernel(tc, x_words, x_scales, w1, near, sharp, of
         x_codes0 = sb.tile([P, S], U32, name="x_codes0", align_bytes=64)
         nc.vector.tensor_copy(x_codes0[:], table_words[0][:].bitcast(U32).indirect(offs_t[:]))
 
-        near_sharp = sb.tile([P, D * V + 1], F32, name="near_sharp", tag="picked_then_near", align_bytes=64)
-        near_t = near_sharp[:, 0 : D * V]
-        sharp_t = near_sharp[:, D * V : D * V + 1]
-        nc.sync.dma_start(out=near_t.rearrange("p (d v) -> p d v", d=D), in_=near.rearrange("d p v -> p d v"))
+        sharp_tile = sb.tile([P, 1], F32, name="sharp_tile", tag="picked_then_near", align_bytes=64)
+        sharp_t = sharp_tile[:]
         nc.sync.dma_start(out=sharp_t, in_=sharp)
+
+        near_cols = psum.tile([P, V // P, P], F32, name="near_cols")
+        for b in range(V // P):
+            nc.tensor.transpose(near_cols[:, b, :], near_rows[:, b * P : (b + 1) * P], identity[:])
+        space_cols = sb.tile([P, V // P, D], F32, name="space_cols")
+        nc.scalar.activation(space_cols[:], near_cols[:, :, 0:D], ACT.Exp)
+        space = psum.tile([P, D * V], F32, name="space")
+        for d in range(D):
+            for b in range(V // P):
+                nc.tensor.transpose(
+                    space[:, d * V + b * P : d * V + (b + 1) * P],
+                    space_cols[:, b, d : d + 1].to_broadcast([P, P]),
+                    identity[:],
+                )
 
         banks = [psum.tile([N, hi - lo], F32, name="bank%d" % lo) for lo, hi in BANK_COLS]
         for bank, (lo, hi) in zip(banks, BANK_COLS):
@@ -88,7 +106,7 @@ def tile_picked_ybilat_sharp_p_kernel(tc, x_words, x_scales, w1, near, sharp, of
                 out=bank[:], lhsT=w_codes[:, 0:N].bitcast(FP8X4), lhsT_scale=w_scales[:, 0:N],
                 rhs=x_codes0[:, lo:hi].bitcast(FP8X4), rhs_scale=x_planes[:, lo:hi], start=True, stop=False,
             )
-        x_codes1 = sb.tile([P, S], U32, name="x_codes1", tag="codes1_then_space", align_bytes=64)
+        x_codes1 = sb.tile([P, S], U32, name="x_codes1", align_bytes=64)
         for lo, hi in ((0, HALF_S), (HALF_S, S)):
             nc.vector.tensor_copy(
                 x_codes1[:, lo:hi],
@@ -102,9 +120,6 @@ def tile_picked_ybilat_sharp_p_kernel(tc, x_words, x_scales, w1, near, sharp, of
                 rhs=x_codes1[:, lo:hi].bitcast(FP8X4), rhs_scale=x_planes[:, S + lo : S + hi], start=False, stop=True,
             )
             copy_out(h[:, lo:hi], bank[:])
-
-        space = sb.tile([P, D * V], F32, name="space", tag="codes1_then_space", align_bytes=64)
-        nc.scalar.activation(space[:], near_t, ACT.Exp)
 
         hc = sb.tile([N, V], F32, name="hc")
         for lo, hi in ((0, HALF_V), (HALF_V, V)):

@@ -19,7 +19,8 @@ ALU = mybir.AluOpType
 P = 128
 PACK = 4
 PASSES = K // (P * PACK)
-QUADS = 4
+QUAD = 32
+QUADS = P // QUAD
 QUAD_ROWS = 4
 SCALE_ROWS = PASSES * QUADS * QUAD_ROWS
 ROW_STEP = P // SCALE_ROWS
@@ -54,21 +55,21 @@ def tile_picked_ybilat_sharp_p_kernel(tc, x_words, x_scales, w1, near, sharp, of
         w_raw = sb.tile([P, PASSES, PACK, N], F32, name="w_raw", align_bytes=64)
 
         nc.sync.dma_start(out=w_raw[:], in_=w1.rearrange("(o p j) n -> p o j n", o=PASSES, j=PACK))
-        nc.sync.dma_start(out=table_scales[0:P:ROW_STEP, :], in_=x_scales.rearrange("o q c -> q o c").bitcast(I32))
         nc.sync.dma_start(offs_t[:], offs)
-        nc.sync.dma_start(out=near_rows[0:D, :], in_=near[:, 0, :])
+        nc.sync.dma_start(out=table_scales[0:P:ROW_STEP, :], in_=x_scales.rearrange("o q c -> q o c").bitcast(I32))
         nc.sync.dma_start(out=table_words[0][:], in_=x_words[0].rearrange("p c r -> p (c r)").bitcast(I32))
+        nc.sync.dma_start(out=near_rows[0:D, :], in_=near[:, 0, :])
         nc.sync.dma_start(out=table_words[1][:], in_=x_words[1].rearrange("p c r -> p (c r)").bitcast(I32))
         nc.sync.dma_start(cen_t[:], cen)
         nc.sync.dma_start(pos_t[0][:], pos1)
         nc.sync.dma_start(pos_t[1][:], pos2)
 
-        picked = sb.tile([P, S], U8, name="picked", tag="picked_then_near", align_bytes=64)
+        picked = sb.tile([P, S], U8, name="picked", tag="picked_then_sharp", align_bytes=64)
         nc.vector.tensor_copy(picked[:], table_scales[:].bitcast(U8).indirect(offs_t[:]))
         for q in range(QUADS):
             nc.scalar.dma_start(
-                out=x_planes[32 * q : 32 * q + QUAD_ROWS, :].rearrange("r (o c) -> r o c", o=PASSES).bitcast(I32),
-                in_=picked[32 * q : 32 * (q + 1) : ROW_STEP, :].bitcast(I32),
+                out=x_planes[QUAD * q : QUAD * q + QUAD_ROWS, :].rearrange("r (o c) -> r o c", o=PASSES).bitcast(I32),
+                in_=picked[QUAD * q : QUAD * (q + 1) : ROW_STEP, :].bitcast(I32),
             )
 
         w_grouped = sb.tile([P, PASSES, N, PACK], BF16, name="w_grouped", align_bytes=64)
@@ -82,23 +83,14 @@ def tile_picked_ybilat_sharp_p_kernel(tc, x_words, x_scales, w1, near, sharp, of
         x_codes0 = sb.tile([P, S], U32, name="x_codes0", align_bytes=64)
         nc.vector.tensor_copy(x_codes0[:], table_words[0][:].bitcast(U32).indirect(offs_t[:]))
 
-        sharp_tile = sb.tile([P, 1], F32, name="sharp_tile", tag="picked_then_near", align_bytes=64)
-        sharp_t = sharp_tile[:]
-        nc.sync.dma_start(out=sharp_t, in_=sharp)
+        sharp_t = sb.tile([P, 1], F32, name="sharp_t", tag="picked_then_sharp", align_bytes=64)
+        nc.sync.dma_start(out=sharp_t[:], in_=sharp)
 
         near_cols = psum.tile([P, V // P, P], F32, name="near_cols")
         for b in range(V // P):
             nc.tensor.transpose(near_cols[:, b, :], near_rows[:, b * P : (b + 1) * P], identity[:])
         space_cols = sb.tile([P, V // P, D], F32, name="space_cols")
         nc.scalar.activation(space_cols[:], near_cols[:, :, 0:D], ACT.Exp)
-        space = psum.tile([P, D * V], F32, name="space")
-        for d in range(D):
-            for b in range(V // P):
-                nc.tensor.transpose(
-                    space[:, d * V + b * P : d * V + (b + 1) * P],
-                    space_cols[:, b, d : d + 1].to_broadcast([P, P]),
-                    identity[:],
-                )
 
         banks = [psum.tile([N, hi - lo], F32, name="bank%d" % lo) for lo, hi in BANK_COLS]
         for bank, (lo, hi) in zip(banks, BANK_COLS):
@@ -121,6 +113,15 @@ def tile_picked_ybilat_sharp_p_kernel(tc, x_words, x_scales, w1, near, sharp, of
             )
             copy_out(h[:, lo:hi], bank[:])
 
+        space = psum.tile([P, D * V], F32, name="space", tag="bank0")
+        for d in range(D):
+            for b in range(V // P):
+                nc.tensor.transpose(
+                    space[:, d * V + b * P : d * V + (b + 1) * P],
+                    space_cols[:, b, d : d + 1].to_broadcast([P, P]),
+                    identity[:],
+                )
+
         hc = sb.tile([N, V], F32, name="hc")
         for lo, hi in ((0, HALF_V), (HALF_V, V)):
             nc.vector.tensor_copy(hc[:, lo:hi], h[:].indirect(cen_t[:, lo // PER_COL : hi // PER_COL]))
@@ -139,7 +140,7 @@ def tile_picked_ybilat_sharp_p_kernel(tc, x_words, x_scales, w1, near, sharp, of
                 nc.vector.tensor_tensor(diff[:, at], looked_up, hc[:, lo:hi], ALU.subtract)
                 if at != last:
                     nc.scalar.activation(diff_sq[:, at], diff[:, at], ACT.Square)
-            nc.scalar.activation(alike[:, exp_cols], diff_sq[:, exp_cols], ACT.Exp, scale=sharp_t)
+            nc.scalar.activation(alike[:, exp_cols], diff_sq[:, exp_cols], ACT.Exp, scale=sharp_t[:])
 
         den = sb.tile([N, V], F32, name="den")
         den_sq = sb.tile([N, HALF_V], F32, name="den_sq")
@@ -152,7 +153,7 @@ def tile_picked_ybilat_sharp_p_kernel(tc, x_words, x_scales, w1, near, sharp, of
 
         nc.vector.scalar_tensor_tensor(far[:, first], diff[:, first], -SHARPEN, hc[:], ALU.mult, ALU.add)
         nc.vector.tensor_tensor(diff_sq[:, last], diff[:, last], diff[:, last], ALU.mult)
-        nc.scalar.activation(alike[:, last], diff_sq[:, last], ACT.Exp, scale=sharp_t)
+        nc.scalar.activation(alike[:, last], diff_sq[:, last], ACT.Exp, scale=sharp_t[:])
         nc.vector.tensor_tensor(wt[:, first], alike[:, first], space[:, first], ALU.mult)
         nc.vector.scalar_tensor_tensor(far[:, second], diff[:, second], -SHARPEN, hc[:], ALU.mult, ALU.add)
         nc.vector.tensor_tensor(wt[:, second], alike[:, second], space[:, second], ALU.mult)

@@ -46,11 +46,12 @@ def tile_picked_ybilat_sharp_p_kernel(tc, x_words, x_scales, w1, near, sharp, of
         table_scales = sb.tile([P, T // 4], I32, name="table_scales", align_bytes=64)
         nc.vector.memset(table_scales[:], 0)
         x_planes = sb.tile([P, PASSES * S], U8, name="x_planes", align_bytes=64)
-        nc.vector.memset(x_planes[:].bitcast(I32), 0)
         near_rows = sb.tile([P, V], F32, name="near_rows")
-        nc.gpsimd.memset(near_rows[:], 0.0)
+        nc.vector.memset(near_rows[:], 0.0)
         identity = sb.tile([P, P], F32, name="identity")
-        make_identity(nc, identity[:])
+        nc.vector.memset(identity[:], 0.0)
+        make_identity(nc, identity[:], nomemset=True)
+        nc.vector.memset(x_planes[:].bitcast(I32), 0)
         table_words = [sb.tile([P, T], I32, name="table_words%d" % o, align_bytes=64) for o in range(PASSES)]
         w_raw = sb.tile([P, PASSES, PACK, N], F32, name="w_raw", align_bytes=64)
 
@@ -133,8 +134,8 @@ def tile_picked_ybilat_sharp_p_kernel(tc, x_words, x_scales, w1, near, sharp, of
         far = sb.tile([N, D * V], F32, name="far")
         first, second = slice(0, V), slice(V, 2 * V)
         body, last = slice(V, 2 * V - LAST), slice(2 * V - LAST, 2 * V)
-        for d, cut, exp_cols in ((0, HALF_V, first), (1, V - LAST, body)):
-            for lo, hi in ((0, cut), (cut, V)):
+        for d, cuts, exp_cols in ((0, (0, HALF_V, V), first), (1, (0, HALF_V, V - LAST, V), body)):
+            for lo, hi in zip(cuts, cuts[1:]):
                 at = slice(d * V + lo, d * V + hi)
                 looked_up = h[:].indirect(pos_t[d][:, lo // PER_COL : hi // PER_COL])
                 nc.vector.tensor_tensor(diff[:, at], looked_up, hc[:, lo:hi], ALU.subtract)
@@ -143,8 +144,8 @@ def tile_picked_ybilat_sharp_p_kernel(tc, x_words, x_scales, w1, near, sharp, of
             nc.scalar.activation(alike[:, exp_cols], diff_sq[:, exp_cols], ACT.Exp, scale=sharp_t[:])
 
         den = sb.tile([N, V], F32, name="den")
-        den_sq = sb.tile([N, HALF_V], F32, name="den_sq")
-        den_rsqrt = sb.tile([N, HALF_V], F32, name="den_rsqrt")
+        den_sq = sb.tile([N, V - LAST], F32, name="den_sq")
+        den_rsqrt = sb.tile([N, LAST], F32, name="den_rsqrt")
         base = sb.tile([N, V], F32, name="base")
         pull1 = sb.tile([N, V], F32, name="pull1")
         top = sb.tile([N, V], F32, name="top")
@@ -161,20 +162,20 @@ def tile_picked_ybilat_sharp_p_kernel(tc, x_words, x_scales, w1, near, sharp, of
         nc.vector.scalar_tensor_tensor(den[:], wt[:, first], 1.0, wt[:, second], ALU.add, ALU.add)
         nc.vector.tensor_tensor(base[:], pull0, hc[:], ALU.add)
 
-        nc.vector.tensor_tensor(den_sq[:], den[:, left], den[:, left], ALU.mult)
-        nc.scalar.activation(den_rsqrt[:], den[:, right], ACT.Abs_reciprocal_sqrt)
+        third, fourth = slice(HALF_V, V - LAST), slice(V - LAST, V)
+        inv_den = sb.tile([N, V], F32, name="inv_den")
+        nc.vector.tensor_tensor(den_sq[:, left], den[:, left], den[:, left], ALU.mult)
+        nc.scalar.activation(den_rsqrt[:], den[:, fourth], ACT.Abs_reciprocal_sqrt)
+        nc.scalar.activation(inv_den[:, left], den_sq[:, left], ACT.Abs_reciprocal_sqrt)
+        nc.scalar.activation(inv_den[:, fourth], den_rsqrt[:], ACT.Square)
         for cols in (left, right):
             at = slice(V + cols.start, V + cols.stop)
             nc.vector.tensor_tensor(pull1[:, cols], wt[:, at], far[:, at], ALU.mult)
+        nc.vector.tensor_tensor(den_sq[:, third], den[:, third], den[:, third], ALU.mult)
+        nc.scalar.activation(inv_den[:, third], den_sq[:, third], ACT.Abs_reciprocal_sqrt)
         for cols in (left, right):
             nc.vector.tensor_tensor(top[:, cols], base[:, cols], pull1[:, cols], ALU.add)
-        halves = (
-            (left, den_sq, ACT.Abs_reciprocal_sqrt, nc.sync),
-            (right, den_rsqrt, ACT.Square, nc.scalar),
-        )
-        for cols, source, func, queue in halves:
-            inv_den = sb.tile([N, HALF_V], F32, name="inv_den%d" % cols.start)
-            nc.scalar.activation(inv_den[:], source[:], func)
+        for cols, queue in ((left, nc.sync), (right, nc.scalar)):
             result = sb.tile([N, HALF_V], F32, name="result%d" % cols.start)
-            nc.vector.tensor_tensor(result[:], top[:, cols], inv_den[:], ALU.mult)
+            nc.vector.tensor_tensor(result[:], top[:, cols], inv_den[:, cols], ALU.mult)
             queue.dma_start(out=out[:, cols], in_=result[:])

@@ -23,7 +23,10 @@ QUAD = 32
 QUADS = P // QUAD
 QUAD_ROWS = 4
 SCALE_ROWS = PASSES * QUADS * QUAD_ROWS
-ROW_STEP = P // SCALE_ROWS
+ROW_STEP = 7
+ROW_AT = 11
+NEAR_AT = 16
+ZERO_SPLIT = 640
 PER_COL = 16
 HALF_S = S // 2
 HALF_V = V // 2
@@ -43,8 +46,9 @@ def tile_picked_ybilat_sharp_p_kernel(tc, x_words, x_scales, w1, near, sharp, of
         cen_t = lists.tile([P, V // PER_COL], U16, name="cen_t")
         pos_t = [lists.tile([P, V // PER_COL], U16, name="pos_t%d" % d) for d in range(D)]
 
-        table_scales = sb.tile([P, T // 4], I32, name="table_scales", align_bytes=64)
-        nc.vector.memset(table_scales[:], 0)
+        table_scales = sb.tile([P, PASSES * T // 4], I32, name="table_scales", align_bytes=64)
+        nc.vector.memset(table_scales[:, 0:ZERO_SPLIT], 0)
+        nc.gpsimd.memset(table_scales[:, ZERO_SPLIT:], 0)
         x_planes = sb.tile([P, PASSES * S], U8, name="x_planes", align_bytes=64)
         near_rows = sb.tile([P, V], F32, name="near_rows")
         nc.vector.memset(near_rows[:], 0.0)
@@ -57,20 +61,26 @@ def tile_picked_ybilat_sharp_p_kernel(tc, x_words, x_scales, w1, near, sharp, of
 
         nc.sync.dma_start(out=w_raw[:], in_=w1.rearrange("(o p j) n -> p o j n", o=PASSES, j=PACK))
         nc.sync.dma_start(offs_t[:], offs)
-        nc.sync.dma_start(out=table_scales[0:P:ROW_STEP, :], in_=x_scales.rearrange("o q c -> q o c").bitcast(I32))
+        nc.sync.dma_start(
+            out=table_scales[ROW_AT : ROW_AT + 15 * ROW_STEP + 1 : ROW_STEP, :].rearrange("q (o c) -> q o c", o=PASSES),
+            in_=x_scales.rearrange("o q c -> q o c").bitcast(I32),
+        )
         nc.sync.dma_start(out=table_words[0][:], in_=x_words[0].rearrange("p c r -> p (c r)").bitcast(I32))
-        nc.sync.dma_start(out=near_rows[0:D, :], in_=near[:, 0, :])
+        nc.sync.dma_start(out=near_rows[NEAR_AT : NEAR_AT + D, :], in_=near[:, 0, :])
         nc.sync.dma_start(out=table_words[1][:], in_=x_words[1].rearrange("p c r -> p (c r)").bitcast(I32))
         nc.sync.dma_start(cen_t[:], cen)
         nc.sync.dma_start(pos_t[0][:], pos1)
         nc.sync.dma_start(pos_t[1][:], pos2)
 
-        picked = sb.tile([P, S], U8, name="picked", tag="picked_then_sharp", align_bytes=64)
-        nc.vector.tensor_copy(picked[:], table_scales[:].bitcast(U8).indirect(offs_t[:]))
-        for q in range(QUADS):
+        picked = sb.tile([P, PASSES * S], U8, name="picked", tag="picked_then_sharp", align_bytes=64)
+        for o in range(PASSES):
+            window = table_scales[:].bitcast(U8)[:, o * T : (o + 1) * T]
+            nc.vector.tensor_copy(picked[:, o * S : (o + 1) * S], window.indirect(offs_t[:]))
+        for r in range(QUAD_ROWS):
+            first_row = ROW_AT + r * ROW_STEP
             nc.scalar.dma_start(
-                out=x_planes[QUAD * q : QUAD * q + QUAD_ROWS, :].rearrange("r (o c) -> r o c", o=PASSES).bitcast(I32),
-                in_=picked[QUAD * q : QUAD * (q + 1) : ROW_STEP, :].bitcast(I32),
+                out=x_planes[r:P:QUAD, :].bitcast(I32),
+                in_=picked[first_row : first_row + 3 * QUAD_ROWS * ROW_STEP + 1 : QUAD_ROWS * ROW_STEP, :].bitcast(I32),
             )
 
         w_grouped = sb.tile([P, PASSES, N, PACK], BF16, name="w_grouped", align_bytes=64)
@@ -91,7 +101,7 @@ def tile_picked_ybilat_sharp_p_kernel(tc, x_words, x_scales, w1, near, sharp, of
         for b in range(V // P):
             nc.tensor.transpose(near_cols[:, b, :], near_rows[:, b * P : (b + 1) * P], identity[:])
         space_cols = sb.tile([P, V // P, D], F32, name="space_cols")
-        nc.scalar.activation(space_cols[:], near_cols[:, :, 0:D], ACT.Exp)
+        nc.scalar.activation(space_cols[:], near_cols[:, :, NEAR_AT : NEAR_AT + D], ACT.Exp)
 
         banks = [psum.tile([N, hi - lo], F32, name="bank%d" % lo) for lo, hi in BANK_COLS]
         for bank, (lo, hi) in zip(banks, BANK_COLS):

@@ -20,19 +20,13 @@ P = 128
 PACK = 4
 PASSES = K // (P * PACK)
 QUAD = 32
-QUADS = P // QUAD
 QUAD_ROWS = 4
-SCALE_ROWS = PASSES * QUADS * QUAD_ROWS
-ROW_STEP = 7
-ROW_AT = 11
-NEAR_AT = 16
-ZERO_SPLIT = 640
+ROW_STEP = 4
+NEAR_AT = 17
 PER_COL = 16
-HALF_S = S // 2
-HALF_V = V // 2
+QUARTER = V // 4
 SHARPEN = 1.5
-BANK_COLS = ((0, HALF_S), (HALF_S, HALF_S + HALF_S // 2), (HALF_S + HALF_S // 2, S))
-LAST = 64
+BANK_COLS = ((0, S // 2), (S // 2, 3 * S // 4), (3 * S // 4, S))
 
 
 def tile_picked_ybilat_sharp_p_kernel(tc, x_words, x_scales, w1, near, sharp, offs, cen, pos1, pos2, out):
@@ -46,25 +40,24 @@ def tile_picked_ybilat_sharp_p_kernel(tc, x_words, x_scales, w1, near, sharp, of
         cen_t = lists.tile([P, V // PER_COL], U16, name="cen_t")
         pos_t = [lists.tile([P, V // PER_COL], U16, name="pos_t%d" % d) for d in range(D)]
 
-        table_scales = sb.tile([P, PASSES * T // 4], I32, name="table_scales", align_bytes=64)
-        nc.vector.memset(table_scales[:, 0:ZERO_SPLIT], 0)
-        nc.gpsimd.memset(table_scales[:, ZERO_SPLIT:], 0)
-        x_planes = sb.tile([P, PASSES * S], U8, name="x_planes", align_bytes=64)
+        def entries(list_t, lo, hi):
+            return list_t[:, lo // PER_COL : hi // PER_COL]
+
+        table_scales = sb.tile([P, T // 4], I32, name="table_scales", align_bytes=64)
+        nc.vector.memset(table_scales[:], 0)
         near_rows = sb.tile([P, V], F32, name="near_rows")
         nc.vector.memset(near_rows[:], 0.0)
+        x_planes = sb.tile([P, PASSES * S], U8, name="x_planes", align_bytes=64)
+        nc.vector.memset(x_planes[:].bitcast(I32), 0)
         identity = sb.tile([P, P], F32, name="identity")
         nc.vector.memset(identity[:], 0.0)
         make_identity(nc, identity[:], nomemset=True)
-        nc.vector.memset(x_planes[:].bitcast(I32), 0)
         table_words = [sb.tile([P, T], I32, name="table_words%d" % o, align_bytes=64) for o in range(PASSES)]
         w_raw = sb.tile([P, PASSES, PACK, N], F32, name="w_raw", align_bytes=64)
 
         nc.sync.dma_start(out=w_raw[:], in_=w1.rearrange("(o p j) n -> p o j n", o=PASSES, j=PACK))
         nc.sync.dma_start(offs_t[:], offs)
-        nc.sync.dma_start(
-            out=table_scales[ROW_AT : ROW_AT + 15 * ROW_STEP + 1 : ROW_STEP, :].rearrange("q (o c) -> q o c", o=PASSES),
-            in_=x_scales.rearrange("o q c -> q o c").bitcast(I32),
-        )
+        nc.sync.dma_start(out=table_scales[0:P:ROW_STEP, :], in_=x_scales.rearrange("o q c -> q o c").bitcast(I32))
         nc.sync.dma_start(out=table_words[0][:], in_=x_words[0].rearrange("p c r -> p (c r)").bitcast(I32))
         nc.sync.dma_start(out=near_rows[NEAR_AT : NEAR_AT + D, :], in_=near[:, 0, :])
         nc.sync.dma_start(out=table_words[1][:], in_=x_words[1].rearrange("p c r -> p (c r)").bitcast(I32))
@@ -72,15 +65,12 @@ def tile_picked_ybilat_sharp_p_kernel(tc, x_words, x_scales, w1, near, sharp, of
         nc.sync.dma_start(pos_t[0][:], pos1)
         nc.sync.dma_start(pos_t[1][:], pos2)
 
-        picked = sb.tile([P, PASSES * S], U8, name="picked", tag="picked_then_sharp", align_bytes=64)
-        for o in range(PASSES):
-            window = table_scales[:].bitcast(U8)[:, o * T : (o + 1) * T]
-            nc.vector.tensor_copy(picked[:, o * S : (o + 1) * S], window.indirect(offs_t[:]))
-        for r in range(QUAD_ROWS):
-            first_row = ROW_AT + r * ROW_STEP
+        picked = sb.tile([P, S], U8, name="picked", tag="picked_then_sharp", align_bytes=64)
+        nc.vector.tensor_copy(picked[:], table_scales[:].bitcast(U8).indirect(offs_t[:]))
+        for q in (0, 2, 1, 3):
             nc.scalar.dma_start(
-                out=x_planes[r:P:QUAD, :].bitcast(I32),
-                in_=picked[first_row : first_row + 3 * QUAD_ROWS * ROW_STEP + 1 : QUAD_ROWS * ROW_STEP, :].bitcast(I32),
+                out=x_planes[q * QUAD : q * QUAD + QUAD_ROWS, :].bitcast(I32),
+                in_=picked[q * QUAD : (q + 1) * QUAD : ROW_STEP, :].bitcast(I32),
             )
 
         w_grouped = sb.tile([P, PASSES, N, PACK], BF16, name="w_grouped", align_bytes=64)
@@ -110,13 +100,10 @@ def tile_picked_ybilat_sharp_p_kernel(tc, x_words, x_scales, w1, near, sharp, of
                 rhs=x_codes0[:, lo:hi].bitcast(FP8X4), rhs_scale=x_planes[:, lo:hi], start=True, stop=False,
             )
         x_codes1 = sb.tile([P, S], U32, name="x_codes1", align_bytes=64)
-        for lo, hi in ((0, HALF_S), (HALF_S, S)):
-            nc.vector.tensor_copy(
-                x_codes1[:, lo:hi],
-                table_words[1][:].bitcast(U32).indirect(offs_t[:, lo // PER_COL : hi // PER_COL]),
-            )
+        for lo, hi in BANK_COLS:
+            nc.vector.tensor_copy(x_codes1[:, lo:hi], table_words[1][:].bitcast(U32).indirect(entries(offs_t, lo, hi)))
         h = sb.tile([N, S], F32, name="h")
-        copies_out = (nc.scalar.copy, nc.vector.tensor_copy, nc.scalar.copy)
+        copies_out = (nc.scalar.copy, nc.scalar.copy, nc.vector.tensor_copy)
         for bank, (lo, hi), copy_out in zip(banks, BANK_COLS, copies_out):
             nc.tensor.matmul_mx(
                 out=bank[:], lhsT=w_codes[:, N : 2 * N].bitcast(FP8X4), lhsT_scale=w_scales[:, N : 2 * N],
@@ -125,67 +112,72 @@ def tile_picked_ybilat_sharp_p_kernel(tc, x_words, x_scales, w1, near, sharp, of
             copy_out(h[:, lo:hi], bank[:])
 
         space = psum.tile([P, D * V], F32, name="space", tag="bank0")
-        for d in range(D):
-            for b in range(V // P):
+        for b in range(V // P):
+            for d in range(D):
                 nc.tensor.transpose(
-                    space[:, d * V + b * P : d * V + (b + 1) * P],
+                    space[:, (b * D + d) * P : (b * D + d + 1) * P],
                     space_cols[:, b, d : d + 1].to_broadcast([P, P]),
                     identity[:],
                 )
 
         hc = sb.tile([N, V], F32, name="hc")
-        for lo, hi in ((0, HALF_V), (HALF_V, V)):
-            nc.vector.tensor_copy(hc[:, lo:hi], h[:].indirect(cen_t[:, lo // PER_COL : hi // PER_COL]))
+        h1 = sb.tile([N, V], F32, name="h1")
+        diff = sb.tile([N, 2, D, P], F32, name="diff")
+        diff_sq = sb.tile([N, 2, D, P], F32, name="diff_sq")
+        alike = sb.tile([N, 2, D, P], F32, name="alike")
+        wt = sb.tile([N, 2, D, P], F32, name="wt")
+        pull = sb.tile([N, 2, D, P], F32, name="pull")
+        halves = (slice(0, P), slice(P, V))
+        q1, q2, q3 = QUARTER, 2 * QUARTER, 3 * QUARTER
 
-        diff = sb.tile([N, D * V], F32, name="diff")
-        diff_sq = sb.tile([N, D * V], F32, name="diff_sq")
-        alike = sb.tile([N, D * V], F32, name="alike")
-        wt = sb.tile([N, D * V], F32, name="wt")
-        far = sb.tile([N, D * V], F32, name="far")
-        first, second = slice(0, V), slice(V, 2 * V)
-        body, last = slice(V, 2 * V - LAST), slice(2 * V - LAST, 2 * V)
-        for d, cuts, exp_cols in ((0, (0, HALF_V, V), first), (1, (0, HALF_V, V - LAST, V), body)):
-            for lo, hi in zip(cuts, cuts[1:]):
-                at = slice(d * V + lo, d * V + hi)
-                looked_up = h[:].indirect(pos_t[d][:, lo // PER_COL : hi // PER_COL])
-                nc.vector.tensor_tensor(diff[:, at], looked_up, hc[:, lo:hi], ALU.subtract)
-                if at != last:
-                    nc.scalar.activation(diff_sq[:, at], diff[:, at], ACT.Square)
-            nc.scalar.activation(alike[:, exp_cols], diff_sq[:, exp_cols], ACT.Exp, scale=sharp_t[:])
+        nc.scalar.activation(hc[:, 0:q1], h[:].indirect(entries(cen_t, 0, q1)), ACT.Copy)
+        for cols in halves:
+            nc.scalar.activation(h1[:, cols], h[:].indirect(entries(pos_t[1], cols.start, cols.stop)), ACT.Copy)
+        for lo, hi in ((q1, q2), (q2, V)):
+            nc.vector.tensor_copy(hc[:, lo:hi], h[:].indirect(entries(cen_t, lo, hi)))
+        for b, cols in enumerate(halves):
+            looked_up = h[:].indirect(entries(pos_t[0], cols.start, cols.stop))
+            nc.vector.tensor_tensor(diff[:, b, 0, :], looked_up, hc[:, cols], ALU.subtract)
+            nc.vector.tensor_tensor(diff[:, b, 1, :], h1[:, cols], hc[:, cols], ALU.subtract)
+        for d in range(D):
+            nc.scalar.activation(diff_sq[:, 0, d, :], diff[:, 0, d, :], ACT.Square)
+            nc.vector.tensor_tensor(diff_sq[:, 1, d, :], diff[:, 1, d, :], diff[:, 1, d, :], ALU.mult)
+        for b in range(2):
+            for d in range(D):
+                nc.scalar.activation(alike[:, b, d, :], diff_sq[:, b, d, :], ACT.Exp, scale=sharp_t[:])
 
+        left, right = halves
+        third, fourth = slice(q2, q3), slice(q3, V)
         den = sb.tile([N, V], F32, name="den")
-        den_sq = sb.tile([N, V - LAST], F32, name="den_sq")
-        den_rsqrt = sb.tile([N, LAST], F32, name="den_rsqrt")
-        base = sb.tile([N, V], F32, name="base")
-        pull1 = sb.tile([N, V], F32, name="pull1")
-        top = sb.tile([N, V], F32, name="top")
-        pull0 = diff_sq[:, second]
-        left, right = slice(0, HALF_V), slice(HALF_V, V)
-
-        nc.vector.scalar_tensor_tensor(far[:, first], diff[:, first], -SHARPEN, hc[:], ALU.mult, ALU.add)
-        nc.vector.tensor_tensor(diff_sq[:, last], diff[:, last], diff[:, last], ALU.mult)
-        nc.scalar.activation(alike[:, last], diff_sq[:, last], ACT.Exp, scale=sharp_t[:])
-        nc.vector.tensor_tensor(wt[:, first], alike[:, first], space[:, first], ALU.mult)
-        nc.vector.scalar_tensor_tensor(far[:, second], diff[:, second], -SHARPEN, hc[:], ALU.mult, ALU.add)
-        nc.vector.tensor_tensor(wt[:, second], alike[:, second], space[:, second], ALU.mult)
-        nc.vector.tensor_tensor(pull0, wt[:, first], far[:, first], ALU.mult)
-        nc.vector.scalar_tensor_tensor(den[:], wt[:, first], 1.0, wt[:, second], ALU.add, ALU.add)
-        nc.vector.tensor_tensor(base[:], pull0, hc[:], ALU.add)
-
-        third, fourth = slice(HALF_V, V - LAST), slice(V - LAST, V)
+        den_sq = sb.tile([N, q3], F32, name="den_sq")
+        den_rsqrt = sb.tile([N, QUARTER], F32, name="den_rsqrt")
         inv_den = sb.tile([N, V], F32, name="inv_den")
-        nc.vector.tensor_tensor(den_sq[:, left], den[:, left], den[:, left], ALU.mult)
+        pulls = sb.tile([N, V], F32, name="pulls")
+        kept = sb.tile([N, V], F32, name="kept")
+        top = sb.tile([N, V], F32, name="top")
+
+        def by_half(tile):
+            return tile[:].rearrange("p (b j) -> p b j", b=2)
+
+        def both(tile, b):
+            return tile[:, b, :, :].rearrange("p d j -> p (d j)")
+
+        for b in range(2):
+            nc.vector.tensor_tensor(both(wt, b), both(alike, b), space[:, b * V : (b + 1) * V], ALU.mult)
+        nc.vector.scalar_tensor_tensor(both(pull, 0), both(diff, 0), -SHARPEN, both(wt, 0), ALU.mult, ALU.mult)
+        nc.vector.scalar_tensor_tensor(by_half(den), wt[:, :, 0, :], 1.0, wt[:, :, 1, :], ALU.add, ALU.add)
+        nc.vector.scalar_tensor_tensor(both(pull, 1), both(diff, 1), -SHARPEN, both(wt, 1), ALU.mult, ALU.mult)
+        nc.vector.tensor_tensor(den_sq[:], den[:, 0:q3], den[:, 0:q3], ALU.mult)
+        nc.vector.tensor_tensor(by_half(pulls), pull[:, :, 0, :], pull[:, :, 1, :], ALU.add)
         nc.scalar.activation(den_rsqrt[:], den[:, fourth], ACT.Abs_reciprocal_sqrt)
         nc.scalar.activation(inv_den[:, left], den_sq[:, left], ACT.Abs_reciprocal_sqrt)
-        nc.scalar.activation(inv_den[:, fourth], den_rsqrt[:], ACT.Square)
-        for cols in (left, right):
-            at = slice(V + cols.start, V + cols.stop)
-            nc.vector.tensor_tensor(pull1[:, cols], wt[:, at], far[:, at], ALU.mult)
-        nc.vector.tensor_tensor(den_sq[:, third], den[:, third], den[:, third], ALU.mult)
         nc.scalar.activation(inv_den[:, third], den_sq[:, third], ACT.Abs_reciprocal_sqrt)
-        for cols in (left, right):
-            nc.vector.tensor_tensor(top[:, cols], base[:, cols], pull1[:, cols], ALU.add)
+        nc.scalar.activation(inv_den[:, fourth], den_rsqrt[:], ACT.Square)
+        for cols in halves:
+            nc.vector.tensor_tensor(kept[:, cols], den[:, cols], hc[:, cols], ALU.mult)
+        for cols in halves:
+            nc.vector.tensor_tensor(top[:, cols], kept[:, cols], pulls[:, cols], ALU.add)
         for cols, queue in ((left, nc.sync), (right, nc.scalar)):
-            result = sb.tile([N, HALF_V], F32, name="result%d" % cols.start)
+            result = sb.tile([N, V // 2], F32, name="result%d" % cols.start)
             nc.vector.tensor_tensor(result[:], top[:, cols], inv_den[:, cols], ALU.mult)
             queue.dma_start(out=out[:, cols], in_=result[:])

@@ -24,7 +24,8 @@ QUAD_ROWS = 4
 ROW_STEP = 4
 NEAR_AT = 17
 PER_COL = 16
-QUARTER = V // 4
+HALF_V = V // 2
+LAST = 64
 SHARPEN = 1.5
 BANK_COLS = ((0, S // 2), (S // 2, 3 * S // 4), (3 * S // 4, S))
 
@@ -112,72 +113,69 @@ def tile_picked_ybilat_sharp_p_kernel(tc, x_words, x_scales, w1, near, sharp, of
             copy_out(h[:, lo:hi], bank[:])
 
         space = psum.tile([P, D * V], F32, name="space", tag="bank0")
-        for b in range(V // P):
-            for d in range(D):
+        for d in range(D):
+            for b in range(V // P):
                 nc.tensor.transpose(
-                    space[:, (b * D + d) * P : (b * D + d + 1) * P],
+                    space[:, d * V + b * P : d * V + (b + 1) * P],
                     space_cols[:, b, d : d + 1].to_broadcast([P, P]),
                     identity[:],
                 )
 
         hc = sb.tile([N, V], F32, name="hc")
-        h1 = sb.tile([N, V], F32, name="h1")
-        diff = sb.tile([N, 2, D, P], F32, name="diff")
-        diff_sq = sb.tile([N, 2, D, P], F32, name="diff_sq")
-        alike = sb.tile([N, 2, D, P], F32, name="alike")
-        wt = sb.tile([N, 2, D, P], F32, name="wt")
-        pull = sb.tile([N, 2, D, P], F32, name="pull")
-        halves = (slice(0, P), slice(P, V))
-        q1, q2, q3 = QUARTER, 2 * QUARTER, 3 * QUARTER
-
-        nc.scalar.activation(hc[:, 0:q1], h[:].indirect(entries(cen_t, 0, q1)), ACT.Copy)
-        for cols in halves:
-            nc.scalar.activation(h1[:, cols], h[:].indirect(entries(pos_t[1], cols.start, cols.stop)), ACT.Copy)
-        for lo, hi in ((q1, q2), (q2, V)):
+        nc.scalar.activation(hc[:, HALF_V:V], h[:].indirect(entries(cen_t, HALF_V, V)), ACT.Copy)
+        h1 = sb.tile([N, HALF_V], F32, name="h1")
+        nc.scalar.activation(h1[:], h[:].indirect(entries(pos_t[1], HALF_V, V)), ACT.Copy)
+        for lo, hi in ((0, LAST), (LAST, HALF_V)):
             nc.vector.tensor_copy(hc[:, lo:hi], h[:].indirect(entries(cen_t, lo, hi)))
-        for b, cols in enumerate(halves):
-            looked_up = h[:].indirect(entries(pos_t[0], cols.start, cols.stop))
-            nc.vector.tensor_tensor(diff[:, b, 0, :], looked_up, hc[:, cols], ALU.subtract)
-            nc.vector.tensor_tensor(diff[:, b, 1, :], h1[:, cols], hc[:, cols], ALU.subtract)
-        for d in range(D):
-            nc.scalar.activation(diff_sq[:, 0, d, :], diff[:, 0, d, :], ACT.Square)
-            nc.vector.tensor_tensor(diff_sq[:, 1, d, :], diff[:, 1, d, :], diff[:, 1, d, :], ALU.mult)
-        for b in range(2):
-            for d in range(D):
-                nc.scalar.activation(alike[:, b, d, :], diff_sq[:, b, d, :], ACT.Exp, scale=sharp_t[:])
 
-        left, right = halves
-        third, fourth = slice(q2, q3), slice(q3, V)
+        diff = sb.tile([N, D * V], F32, name="diff")
+        diff_sq = sb.tile([N, D * V], F32, name="diff_sq")
+        alike = sb.tile([N, D * V], F32, name="alike")
+        wt = sb.tile([N, D * V], F32, name="wt")
+        far = sb.tile([N, D * V], F32, name="far")
+        first, second = slice(0, V), slice(V, 2 * V)
+        body, last = slice(V, V + HALF_V), slice(V + HALF_V, 2 * V)
+        for d, cuts, exp_cols in ((0, (0, LAST, HALF_V, V), first), (1, (0, HALF_V), body)):
+            for lo, hi in zip(cuts, cuts[1:]):
+                at = slice(d * V + lo, d * V + hi)
+                looked_up = h[:].indirect(pos_t[d][:, lo // PER_COL : hi // PER_COL])
+                nc.vector.tensor_tensor(diff[:, at], looked_up, hc[:, lo:hi], ALU.subtract)
+                nc.scalar.activation(diff_sq[:, at], diff[:, at], ACT.Square)
+            nc.scalar.activation(alike[:, exp_cols], diff_sq[:, exp_cols], ACT.Exp, scale=sharp_t[:])
+
+        nc.vector.tensor_tensor(diff[:, last], h1[:], hc[:, HALF_V:V], ALU.subtract)
+
         den = sb.tile([N, V], F32, name="den")
-        den_sq = sb.tile([N, q3], F32, name="den_sq")
-        den_rsqrt = sb.tile([N, QUARTER], F32, name="den_rsqrt")
-        inv_den = sb.tile([N, V], F32, name="inv_den")
-        pulls = sb.tile([N, V], F32, name="pulls")
-        kept = sb.tile([N, V], F32, name="kept")
+        den_sq = sb.tile([N, V - LAST], F32, name="den_sq")
+        den_rsqrt = sb.tile([N, LAST], F32, name="den_rsqrt")
+        base = sb.tile([N, V], F32, name="base")
+        pull1 = sb.tile([N, V], F32, name="pull1")
         top = sb.tile([N, V], F32, name="top")
+        pull0 = sb.tile([N, V], F32, name="pull0")
+        left, right = slice(0, HALF_V), slice(HALF_V, V)
+        third, fourth = slice(HALF_V, V - LAST), slice(V - LAST, V)
+        inv_den = sb.tile([N, V], F32, name="inv_den")
 
-        def by_half(tile):
-            return tile[:].rearrange("p (b j) -> p b j", b=2)
-
-        def both(tile, b):
-            return tile[:, b, :, :].rearrange("p d j -> p (d j)")
-
-        for b in range(2):
-            nc.vector.tensor_tensor(both(wt, b), both(alike, b), space[:, b * V : (b + 1) * V], ALU.mult)
-        nc.vector.scalar_tensor_tensor(both(pull, 0), both(diff, 0), -SHARPEN, both(wt, 0), ALU.mult, ALU.mult)
-        nc.vector.scalar_tensor_tensor(by_half(den), wt[:, :, 0, :], 1.0, wt[:, :, 1, :], ALU.add, ALU.add)
-        nc.vector.scalar_tensor_tensor(both(pull, 1), both(diff, 1), -SHARPEN, both(wt, 1), ALU.mult, ALU.mult)
-        nc.vector.tensor_tensor(den_sq[:], den[:, 0:q3], den[:, 0:q3], ALU.mult)
-        nc.vector.tensor_tensor(by_half(pulls), pull[:, :, 0, :], pull[:, :, 1, :], ALU.add)
+        nc.vector.scalar_tensor_tensor(far[:, first], diff[:, first], -SHARPEN, hc[:], ALU.mult, ALU.add)
+        nc.vector.tensor_tensor(diff_sq[:, last], diff[:, last], diff[:, last], ALU.mult)
+        nc.scalar.activation(alike[:, last], diff_sq[:, last], ACT.Exp, scale=sharp_t[:])
+        nc.vector.tensor_tensor(wt[:, first], alike[:, first], space[:, first], ALU.mult)
+        nc.vector.scalar_tensor_tensor(far[:, second], diff[:, second], -SHARPEN, hc[:], ALU.mult, ALU.add)
+        nc.vector.tensor_tensor(pull0[:], wt[:, first], far[:, first], ALU.mult)
+        nc.vector.tensor_tensor(wt[:, second], alike[:, second], space[:, second], ALU.mult)
+        nc.vector.tensor_tensor(base[:], pull0[:], hc[:], ALU.add)
+        nc.vector.scalar_tensor_tensor(den[:], wt[:, first], 1.0, wt[:, second], ALU.add, ALU.add)
+        nc.vector.tensor_tensor(pull1[:, left], wt[:, body], far[:, body], ALU.mult)
+        nc.vector.tensor_tensor(den_sq[:, left], den[:, left], den[:, left], ALU.mult)
+        nc.vector.tensor_tensor(pull1[:, right], wt[:, last], far[:, last], ALU.mult)
+        nc.vector.tensor_tensor(den_sq[:, third], den[:, third], den[:, third], ALU.mult)
         nc.scalar.activation(den_rsqrt[:], den[:, fourth], ACT.Abs_reciprocal_sqrt)
         nc.scalar.activation(inv_den[:, left], den_sq[:, left], ACT.Abs_reciprocal_sqrt)
-        nc.scalar.activation(inv_den[:, third], den_sq[:, third], ACT.Abs_reciprocal_sqrt)
         nc.scalar.activation(inv_den[:, fourth], den_rsqrt[:], ACT.Square)
-        for cols in halves:
-            nc.vector.tensor_tensor(kept[:, cols], den[:, cols], hc[:, cols], ALU.mult)
-        for cols in halves:
-            nc.vector.tensor_tensor(top[:, cols], kept[:, cols], pulls[:, cols], ALU.add)
+        nc.scalar.activation(inv_den[:, third], den_sq[:, third], ACT.Abs_reciprocal_sqrt)
+        for cols in (left, right):
+            nc.vector.tensor_tensor(top[:, cols], base[:, cols], pull1[:, cols], ALU.add)
         for cols, queue in ((left, nc.sync), (right, nc.scalar)):
-            result = sb.tile([N, V // 2], F32, name="result%d" % cols.start)
+            result = sb.tile([N, HALF_V], F32, name="result%d" % cols.start)
             nc.vector.tensor_tensor(result[:], top[:, cols], inv_den[:, cols], ALU.mult)
             queue.dma_start(out=out[:, cols], in_=result[:])

@@ -122,60 +122,110 @@ def tile_picked_ybilat_sharp_p_kernel(tc, x_words, x_scales, w1, near, sharp, of
                 )
 
         hc = sb.tile([N, V], F32, name="hc")
-        nc.scalar.activation(hc[:, HALF_V:V], h[:].indirect(entries(cen_t, HALF_V, V)), ACT.Copy)
         h1 = sb.tile([N, HALF_V], F32, name="h1")
-        nc.scalar.activation(h1[:], h[:].indirect(entries(pos_t[1], HALF_V, V)), ACT.Copy)
-        for lo, hi in ((0, LAST), (LAST, HALF_V)):
-            nc.vector.tensor_copy(hc[:, lo:hi], h[:].indirect(entries(cen_t, lo, hi)))
-
         diff = sb.tile([N, D * V], F32, name="diff")
         diff_sq = sb.tile([N, D * V], F32, name="diff_sq")
         alike = sb.tile([N, D * V], F32, name="alike")
         wt = sb.tile([N, D * V], F32, name="wt")
         far = sb.tile([N, D * V], F32, name="far")
-        first, second = slice(0, V), slice(V, 2 * V)
-        body, last = slice(V, V + HALF_V), slice(V + HALF_V, 2 * V)
-        for d, cuts, exp_cols in ((0, (0, LAST, HALF_V, V), first), (1, (0, HALF_V), body)):
-            for lo, hi in zip(cuts, cuts[1:]):
-                at = slice(d * V + lo, d * V + hi)
-                looked_up = h[:].indirect(pos_t[d][:, lo // PER_COL : hi // PER_COL])
-                nc.vector.tensor_tensor(diff[:, at], looked_up, hc[:, lo:hi], ALU.subtract)
-                nc.scalar.activation(diff_sq[:, at], diff[:, at], ACT.Square)
-            nc.scalar.activation(alike[:, exp_cols], diff_sq[:, exp_cols], ACT.Exp, scale=sharp_t[:])
-
-        nc.vector.tensor_tensor(diff[:, last], h1[:], hc[:, HALF_V:V], ALU.subtract)
-
+        pull = sb.tile([N, D * V], F32, name="pull")
         den = sb.tile([N, V], F32, name="den")
-        den_sq = sb.tile([N, V - LAST], F32, name="den_sq")
-        den_rsqrt = sb.tile([N, LAST], F32, name="den_rsqrt")
-        base = sb.tile([N, V], F32, name="base")
-        pull1 = sb.tile([N, V], F32, name="pull1")
-        top = sb.tile([N, V], F32, name="top")
-        pull0 = sb.tile([N, V], F32, name="pull0")
-        left, right = slice(0, HALF_V), slice(HALF_V, V)
-        third, fourth = slice(HALF_V, V - LAST), slice(V - LAST, V)
+        den_sq = sb.tile([N, V], F32, name="den_sq")
+        den_rsqrt = sb.tile([N, V], F32, name="den_rsqrt")
         inv_den = sb.tile([N, V], F32, name="inv_den")
+        base = sb.tile([N, V], F32, name="base")
+        top = sb.tile([N, V], F32, name="top")
+        result = sb.tile([N, V], F32, name="result")
+        q1, q2, q3 = V // 4, V // 2, 3 * V // 4
 
-        nc.vector.scalar_tensor_tensor(far[:, first], diff[:, first], -SHARPEN, hc[:], ALU.mult, ALU.add)
-        nc.vector.tensor_tensor(diff_sq[:, last], diff[:, last], diff[:, last], ALU.mult)
-        nc.scalar.activation(alike[:, last], diff_sq[:, last], ACT.Exp, scale=sharp_t[:])
-        nc.vector.tensor_tensor(wt[:, first], alike[:, first], space[:, first], ALU.mult)
-        nc.vector.scalar_tensor_tensor(far[:, second], diff[:, second], -SHARPEN, hc[:], ALU.mult, ALU.add)
-        nc.vector.tensor_tensor(pull0[:], wt[:, first], far[:, first], ALU.mult)
-        nc.vector.tensor_tensor(wt[:, second], alike[:, second], space[:, second], ALU.mult)
-        nc.vector.tensor_tensor(base[:], pull0[:], hc[:], ALU.add)
-        nc.vector.scalar_tensor_tensor(den[:], wt[:, first], 1.0, wt[:, second], ALU.add, ALU.add)
-        nc.vector.tensor_tensor(pull1[:, left], wt[:, body], far[:, body], ALU.mult)
-        nc.vector.tensor_tensor(den_sq[:, left], den[:, left], den[:, left], ALU.mult)
-        nc.vector.tensor_tensor(pull1[:, right], wt[:, last], far[:, last], ALU.mult)
-        nc.vector.tensor_tensor(den_sq[:, third], den[:, third], den[:, third], ALU.mult)
-        nc.scalar.activation(den_rsqrt[:], den[:, fourth], ACT.Abs_reciprocal_sqrt)
-        nc.scalar.activation(inv_den[:, left], den_sq[:, left], ACT.Abs_reciprocal_sqrt)
-        nc.scalar.activation(inv_den[:, fourth], den_rsqrt[:], ACT.Square)
-        nc.scalar.activation(inv_den[:, third], den_sq[:, third], ACT.Abs_reciprocal_sqrt)
-        for cols in (left, right):
-            nc.vector.tensor_tensor(top[:, cols], base[:, cols], pull1[:, cols], ALU.add)
-        for cols, queue in ((left, nc.sync), (right, nc.scalar)):
-            result = sb.tile([N, HALF_V], F32, name="result%d" % cols.start)
-            nc.vector.tensor_tensor(result[:], top[:, cols], inv_den[:, cols], ALU.mult)
-            queue.dma_start(out=out[:, cols], in_=result[:])
+        def of(tile, d, lo, hi):
+            return tile[:, d * V + lo : d * V + hi]
+
+        def centre_on_scalar(lo, hi):
+            nc.scalar.activation(hc[:, lo:hi], h[:].indirect(entries(cen_t, lo, hi)), ACT.Copy)
+
+        def centre_on_vector(lo, hi):
+            nc.vector.tensor_copy(hc[:, lo:hi], h[:].indirect(entries(cen_t, lo, hi)))
+
+        def look_up_diff(d, lo, hi):
+            nc.vector.tensor_tensor(of(diff, d, lo, hi), h[:].indirect(entries(pos_t[d], lo, hi)), hc[:, lo:hi], ALU.subtract)
+
+        def square_on_scalar(d, lo, hi):
+            nc.scalar.activation(of(diff_sq, d, lo, hi), of(diff, d, lo, hi), ACT.Square)
+
+        def square_on_vector(d, lo, hi):
+            nc.vector.tensor_tensor(of(diff_sq, d, lo, hi), of(diff, d, lo, hi), of(diff, d, lo, hi), ALU.mult)
+
+        def range_weight(d, lo, hi):
+            nc.scalar.activation(of(alike, d, lo, hi), of(diff_sq, d, lo, hi), ACT.Exp, scale=sharp_t[:])
+
+        def make_far(d, lo, hi):
+            nc.vector.scalar_tensor_tensor(of(far, d, lo, hi), of(diff, d, lo, hi), -SHARPEN, hc[:, lo:hi], ALU.mult, ALU.add)
+
+        def weight(d, lo, hi):
+            nc.vector.tensor_tensor(of(wt, d, lo, hi), of(alike, d, lo, hi), of(space, d, lo, hi), ALU.mult)
+
+        def make_pull(d, lo, hi):
+            nc.vector.tensor_tensor(of(pull, d, lo, hi), of(wt, d, lo, hi), of(far, d, lo, hi), ALU.mult)
+
+        def make_den(lo, hi):
+            nc.vector.scalar_tensor_tensor(den[:, lo:hi], of(wt, 0, lo, hi), 1.0, of(wt, 1, lo, hi), ALU.add, ALU.add)
+
+        def square_den(lo, hi):
+            nc.vector.tensor_tensor(den_sq[:, lo:hi], den[:, lo:hi], den[:, lo:hi], ALU.mult)
+
+        def make_base(lo, hi):
+            nc.vector.tensor_tensor(base[:, lo:hi], of(pull, 0, lo, hi), hc[:, lo:hi], ALU.add)
+
+        def make_top(lo, hi):
+            nc.vector.tensor_tensor(top[:, lo:hi], base[:, lo:hi], of(pull, 1, lo, hi), ALU.add)
+
+        def invert(lo, hi):
+            nc.scalar.activation(inv_den[:, lo:hi], den_sq[:, lo:hi], ACT.Abs_reciprocal_sqrt)
+
+        def root(lo, hi):
+            nc.scalar.activation(den_rsqrt[:, lo:hi], den[:, lo:hi], ACT.Abs_reciprocal_sqrt)
+
+        def square_root(lo, hi):
+            nc.scalar.activation(inv_den[:, lo:hi], den_rsqrt[:, lo:hi], ACT.Square)
+
+        def finish(lo, hi, queue):
+            nc.vector.tensor_tensor(result[:, lo:hi], top[:, lo:hi], inv_den[:, lo:hi], ALU.mult)
+            queue.dma_start(out=out[:, lo:hi], in_=result[:, lo:hi])
+
+        centre_on_scalar(q2, V)
+        nc.scalar.activation(h1[:], h[:].indirect(entries(pos_t[1], q2, V)), ACT.Copy)
+        centre_on_vector(0, q1)
+        centre_on_vector(q1, q2)
+        look_up_diff(0, 0, q1)
+        look_up_diff(0, q1, q2)
+        look_up_diff(0, q2, V)
+        look_up_diff(1, 0, q2)
+        nc.vector.tensor_tensor(of(diff, 1, q2, V), h1[:], hc[:, q2:V], ALU.subtract)
+        square_on_scalar(0, 0, q1)
+        square_on_scalar(0, q1, q2)
+        square_on_scalar(0, q2, V)
+        range_weight(0, 0, V)
+        square_on_scalar(1, 0, q2)
+        range_weight(1, 0, q2)
+        make_far(0, 0, V)
+        square_on_vector(1, q2, V)
+        range_weight(1, q2, V)
+        weight(0, 0, V)
+        make_far(1, 0, V)
+        make_pull(0, 0, V)
+        weight(1, 0, V)
+        make_base(0, V)
+        make_den(0, V)
+        make_pull(1, 0, q2)
+        square_den(0, q2)
+        make_pull(1, q2, V)
+        square_den(q2, q3)
+        root(q3, V)
+        invert(0, q2)
+        square_root(q3, V)
+        invert(q2, q3)
+        make_top(0, q2)
+        make_top(q2, V)
+        finish(0, q2, nc.sync)
+        finish(q2, V, nc.scalar)

@@ -68,8 +68,8 @@ def tile_picked_ybilat_sharp_p_kernel(tc, x_words, x_scales, w1, near, sharp, of
 
         picked = sb.tile([P, S], U8, name="picked", tag="picked_then_sharp", align_bytes=64)
         nc.vector.tensor_copy(picked[:], table_scales[:].bitcast(U8).indirect(offs_t[:]))
-        for q in (0, 2, 1, 3):
-            nc.scalar.dma_start(
+        for q, queue in ((0, nc.sync), (2, nc.scalar), (1, nc.sync), (3, nc.scalar)):
+            queue.dma_start(
                 out=x_planes[q * QUAD : q * QUAD + QUAD_ROWS, :].bitcast(I32),
                 in_=picked[q * QUAD : (q + 1) * QUAD : ROW_STEP, :].bitcast(I32),
             )
@@ -227,5 +227,5 @@ def tile_picked_ybilat_sharp_p_kernel(tc, x_words, x_scales, w1, near, sharp, of
         invert(q2, q3)
         make_top(0, q2)
         make_top(q2, V)
-        finish(0, q2, nc.sync)
+        finish(0, q2, nc.scalar)
         finish(q2, V, nc.scalar)

@@ -25,7 +25,6 @@ ROW_STEP = 4
 NEAR_AT = 17
 PER_COL = 16
 HALF_V = V // 2
-LAST = 64
 SHARPEN = 1.5
 BANK_COLS = ((0, S // 2), (S // 2, 3 * S // 4), (3 * S // 4, S))
 
@@ -68,8 +67,8 @@ def tile_picked_ybilat_sharp_p_kernel(tc, x_words, x_scales, w1, near, sharp, of
 
         picked = sb.tile([P, S], U8, name="picked", tag="picked_then_sharp", align_bytes=64)
         nc.vector.tensor_copy(picked[:], table_scales[:].bitcast(U8).indirect(offs_t[:]))
-        for q, queue in ((0, nc.sync), (2, nc.scalar), (1, nc.sync), (3, nc.scalar)):
-            queue.dma_start(
+        for q in (0, 2, 1, 3):
+            nc.scalar.dma_start(
                 out=x_planes[q * QUAD : q * QUAD + QUAD_ROWS, :].bitcast(I32),
                 in_=picked[q * QUAD : (q + 1) * QUAD : ROW_STEP, :].bitcast(I32),
             )
@@ -104,7 +103,7 @@ def tile_picked_ybilat_sharp_p_kernel(tc, x_words, x_scales, w1, near, sharp, of
         for lo, hi in BANK_COLS:
             nc.vector.tensor_copy(x_codes1[:, lo:hi], table_words[1][:].bitcast(U32).indirect(entries(offs_t, lo, hi)))
         h = sb.tile([N, S], F32, name="h")
-        copies_out = (nc.scalar.copy, nc.scalar.copy, nc.vector.tensor_copy)
+        copies_out = (nc.scalar.copy, nc.vector.tensor_copy, nc.scalar.copy)
         for bank, (lo, hi), copy_out in zip(banks, BANK_COLS, copies_out):
             nc.tensor.matmul_mx(
                 out=bank[:], lhsT=w_codes[:, N : 2 * N].bitcast(FP8X4), lhsT_scale=w_scales[:, N : 2 * N],
@@ -136,7 +135,7 @@ def tile_picked_ybilat_sharp_p_kernel(tc, x_words, x_scales, w1, near, sharp, of
         base = sb.tile([N, V], F32, name="base")
         top = sb.tile([N, V], F32, name="top")
         result = sb.tile([N, V], F32, name="result")
-        q1, q2, q3 = V // 4, V // 2, 3 * V // 4
+        q1, q2 = V // 4, V // 2
 
         def of(tile, d, lo, hi):
             return tile[:, d * V + lo : d * V + hi]
@@ -202,8 +201,7 @@ def tile_picked_ybilat_sharp_p_kernel(tc, x_words, x_scales, w1, near, sharp, of
         look_up_diff(0, q2, V)
         look_up_diff(1, 0, q2)
         nc.vector.tensor_tensor(of(diff, 1, q2, V), h1[:], hc[:, q2:V], ALU.subtract)
-        square_on_scalar(0, 0, q1)
-        square_on_scalar(0, q1, q2)
+        square_on_scalar(0, 0, q2)
         square_on_scalar(0, q2, V)
         range_weight(0, 0, V)
         square_on_scalar(1, 0, q2)
@@ -220,11 +218,9 @@ def tile_picked_ybilat_sharp_p_kernel(tc, x_words, x_scales, w1, near, sharp, of
         make_pull(1, 0, q2)
         square_den(0, q2)
         make_pull(1, q2, V)
-        square_den(q2, q3)
-        root(q3, V)
+        root(q2, V)
         invert(0, q2)
-        square_root(q3, V)
-        invert(q2, q3)
+        square_root(q2, V)
         make_top(0, q2)
         make_top(q2, V)
         finish(0, q2, nc.scalar)

@@ -43,7 +43,7 @@ def tile_picked_ybilat_sharp_p_kernel(tc, x_words, x_scales, w1, near, sharp, of
         def entries(list_t, lo, hi):
             return list_t[:, lo // PER_COL : hi // PER_COL]
 
-        table_scales = sb.tile([P, T // 4], I32, name="table_scales", align_bytes=64)
+        table_scales = sb.tile([P, T // 4], I32, name="table_scales", align_bytes=256)
         nc.vector.memset(table_scales[:], 0)
         near_rows = sb.tile([P, V], F32, name="near_rows")
         nc.vector.memset(near_rows[:], 0.0)
@@ -52,8 +52,8 @@ def tile_picked_ybilat_sharp_p_kernel(tc, x_words, x_scales, w1, near, sharp, of
         identity = sb.tile([P, P], F32, name="identity")
         nc.vector.memset(identity[:], 0.0)
         make_identity(nc, identity[:], nomemset=True)
-        table_words = [sb.tile([P, T], I32, name="table_words%d" % o, align_bytes=64) for o in range(PASSES)]
-        w_raw = sb.tile([P, PASSES, PACK, N], F32, name="w_raw", align_bytes=64)
+        table_words = [sb.tile([P, T], I32, name="table_words%d" % o, align_bytes=256) for o in range(PASSES)]
+        w_raw = sb.tile([P, PASSES, PACK, N], F32, name="w_raw", align_bytes=256)
 
         nc.sync.dma_start(out=w_raw[:], in_=w1.rearrange("(o p j) n -> p o j n", o=PASSES, j=PACK))
         nc.sync.dma_start(offs_t[:], offs)

@@ -45,9 +45,9 @@ def tile_picked_ybilat_sharp_p_kernel(tc, x_words, x_scales, w1, near, sharp, of
 
         table_scales = sb.tile([P, T // 4], I32, name="table_scales", align_bytes=256)
         nc.vector.memset(table_scales[:], 0)
-        near_rows = sb.tile([P, V], F32, name="near_rows")
+        near_rows = sb.tile([P, V], F32, name="near_rows", align_bytes=256)
         nc.vector.memset(near_rows[:], 0.0)
-        x_planes = sb.tile([P, PASSES * S], U8, name="x_planes", align_bytes=64)
+        x_planes = sb.tile([P, PASSES * S], U8, name="x_planes", align_bytes=256)
         nc.vector.memset(x_planes[:].bitcast(I32), 0)
         identity = sb.tile([P, P], F32, name="identity")
         nc.vector.memset(identity[:], 0.0)
@@ -65,7 +65,7 @@ def tile_picked_ybilat_sharp_p_kernel(tc, x_words, x_scales, w1, near, sharp, of
         nc.sync.dma_start(pos_t[0][:], pos1)
         nc.sync.dma_start(pos_t[1][:], pos2)
 
-        picked = sb.tile([P, S], U8, name="picked", tag="picked_then_sharp", align_bytes=64)
+        picked = sb.tile([P, S], U8, name="picked", tag="picked_then_sharp", align_bytes=256)
         nc.vector.tensor_copy(picked[:], table_scales[:].bitcast(U8).indirect(offs_t[:]))
         for q in (0, 2, 1, 3):
             nc.scalar.dma_start(
@@ -84,7 +84,7 @@ def tile_picked_ybilat_sharp_p_kernel(tc, x_words, x_scales, w1, near, sharp, of
         x_codes0 = sb.tile([P, S], U32, name="x_codes0", align_bytes=64)
         nc.vector.tensor_copy(x_codes0[:], table_words[0][:].bitcast(U32).indirect(offs_t[:]))
 
-        sharp_t = sb.tile([P, 1], F32, name="sharp_t", tag="picked_then_sharp", align_bytes=64)
+        sharp_t = sb.tile([P, 1], F32, name="sharp_t", tag="picked_then_sharp", align_bytes=256)
         nc.sync.dma_start(out=sharp_t[:], in_=sharp)
 
         near_cols = psum.tile([P, V // P, P], F32, name="near_cols")
@@ -134,7 +134,7 @@ def tile_picked_ybilat_sharp_p_kernel(tc, x_words, x_scales, w1, near, sharp, of
         inv_den = sb.tile([N, V], F32, name="inv_den")
         base = sb.tile([N, V], F32, name="base")
         top = sb.tile([N, V], F32, name="top")
-        result = sb.tile([N, V], F32, name="result")
+        result = sb.tile([N, V], F32, name="result", align_bytes=256)
         q1, q2 = V // 4, V // 2
 
         def of(tile, d, lo, hi):

@@ -209,12 +209,12 @@ def tile_picked_ybilat_sharp_p_kernel(tc, x_words, x_scales, w1, near, sharp, of
         make_far(0, 0, V)
         square_on_vector(1, q2, V)
         range_weight(1, q2, V)
-        weight(0, 0, V)
         make_far(1, 0, V)
-        make_pull(0, 0, V)
+        weight(0, 0, V)
         weight(1, 0, V)
-        make_base(0, V)
+        make_pull(0, 0, V)
         make_den(0, V)
+        make_base(0, V)
         make_pull(1, 0, q2)
         square_den(0, q2)
         make_pull(1, q2, V)

from contextlib import ExitStack

import concourse.mybir as mybir
from concourse.masks import make_identity

K, T, S, V, N, D = 1024, 2048, 512, 256, 128, 2
FLOPS = 2 * K * S * N

F32 = mybir.dt.float32
BF16 = mybir.dt.bfloat16
I32 = mybir.dt.int32
U32 = mybir.dt.uint32
U16 = mybir.dt.uint16
U8 = mybir.dt.uint8
FP8X4 = mybir.dt.float8_e4m3fn_x4
ACT = mybir.ActivationFunctionType
ALU = mybir.AluOpType

P = 128
PACK = 4
PASSES = K // (P * PACK)
QUAD = 32
QUAD_ROWS = 4
ROW_STEP = 4
NEAR_AT = 17
PER_COL = 16
HALF_V = V // 2
SHARPEN = 1.5
BANK_COLS = ((0, S // 2), (S // 2, 3 * S // 4), (3 * S // 4, S))


def tile_picked_ybilat_sharp_p_kernel(tc, x_words, x_scales, w1, near, sharp, offs, cen, pos1, pos2, out):
    nc = tc.nc
    with ExitStack() as ctx:
        lists = ctx.enter_context(tc.tile_pool(name="lists", bufs=1))
        sb = ctx.enter_context(tc.tile_pool(name="sb", bufs=1))
        psum = ctx.enter_context(tc.psum_pool(name="psum", bufs=1))

        offs_t = lists.tile([P, S // PER_COL], U16, name="offs_t")
        cen_t = lists.tile([P, V // PER_COL], U16, name="cen_t")
        pos_t = [lists.tile([P, V // PER_COL], U16, name="pos_t%d" % d) for d in range(D)]

        def entries(list_t, lo, hi):
            return list_t[:, lo // PER_COL : hi // PER_COL]

        table_scales = sb.tile([P, T // 4], I32, name="table_scales", align_bytes=256)
        nc.vector.memset(table_scales[:], 0)
        near_rows = sb.tile([P, V], F32, name="near_rows", align_bytes=256)
        nc.vector.memset(near_rows[:], 0.0)
        x_planes = sb.tile([P, PASSES * S], U8, name="x_planes", align_bytes=256)
        nc.vector.memset(x_planes[:].bitcast(I32), 0)
        identity = sb.tile([P, P], F32, name="identity")
        nc.vector.memset(identity[:], 0.0)
        make_identity(nc, identity[:], nomemset=True)
        table_words = [sb.tile([P, T], I32, name="table_words%d" % o, align_bytes=256) for o in range(PASSES)]
        w_raw = sb.tile([P, PASSES, PACK, N], F32, name="w_raw", align_bytes=256)

        nc.sync.dma_start(out=w_raw[:], in_=w1.rearrange("(o p j) n -> p o j n", o=PASSES, j=PACK))
        nc.sync.dma_start(offs_t[:], offs)
        nc.sync.dma_start(out=table_scales[0:P:ROW_STEP, :], in_=x_scales.rearrange("o q c -> q o c").bitcast(I32))
        nc.sync.dma_start(out=table_words[0][:], in_=x_words[0].rearrange("p c r -> p (c r)").bitcast(I32))
        nc.sync.dma_start(out=near_rows[NEAR_AT : NEAR_AT + D, :], in_=near[:, 0, :])
        nc.sync.dma_start(out=table_words[1][:], in_=x_words[1].rearrange("p c r -> p (c r)").bitcast(I32))
        nc.sync.dma_start(cen_t[:], cen)
        nc.sync.dma_start(pos_t[0][:], pos1)
        nc.sync.dma_start(pos_t[1][:], pos2)

        picked = sb.tile([P, S], U8, name="picked", tag="picked_then_sharp", align_bytes=256)
        nc.vector.tensor_copy(picked[:], table_scales[:].bitcast(U8).indirect(offs_t[:]))
        for q in (0, 2, 1, 3):
            nc.scalar.dma_start(
                out=x_planes[q * QUAD : q * QUAD + QUAD_ROWS, :].bitcast(I32),
                in_=picked[q * QUAD : (q + 1) * QUAD : ROW_STEP, :].bitcast(I32),
            )

        w_grouped = sb.tile([P, PASSES, N, PACK], BF16, name="w_grouped", align_bytes=64)
        nc.scalar.copy(w_grouped[:], w_raw[:].rearrange("p o j n -> p o n j"))
        w_codes = sb.tile([P, PASSES * N], U32, name="w_codes", align_bytes=64)
        w_scales = sb.tile([P, PASSES * N], U8, name="w_scales", align_bytes=64)
        nc.vector.quantize_mx(
            out=w_codes[:].bitcast(FP8X4), scales=w_scales[:], in_=w_grouped[:].rearrange("p o n j -> p (o n j)")
        )

        x_codes0 = sb.tile([P, S], U32, name="x_codes0", align_bytes=64)
        nc.vector.tensor_copy(x_codes0[:], table_words[0][:].bitcast(U32).indirect(offs_t[:]))

        sharp_t = sb.tile([P, 1], F32, name="sharp_t", tag="picked_then_sharp", align_bytes=256)
        nc.sync.dma_start(out=sharp_t[:], in_=sharp)

        near_cols = psum.tile([P, V // P, P], F32, name="near_cols")
        for b in range(V // P):
            nc.tensor.transpose(near_cols[:, b, :], near_rows[:, b * P : (b + 1) * P], identity[:])
        space_cols = sb.tile([P, V // P, D], F32, name="space_cols")
        nc.scalar.activation(space_cols[:], near_cols[:, :, NEAR_AT : NEAR_AT + D], ACT.Exp)

        banks = [psum.tile([N, hi - lo], F32, name="bank%d" % lo) for lo, hi in BANK_COLS]
        for bank, (lo, hi) in zip(banks, BANK_COLS):
            nc.tensor.matmul_mx(
                out=bank[:], lhsT=w_codes[:, 0:N].bitcast(FP8X4), lhsT_scale=w_scales[:, 0:N],
                rhs=x_codes0[:, lo:hi].bitcast(FP8X4), rhs_scale=x_planes[:, lo:hi], start=True, stop=False,
            )
        x_codes1 = sb.tile([P, S], U32, name="x_codes1", align_bytes=64)
        for lo, hi in BANK_COLS:
            nc.vector.tensor_copy(x_codes1[:, lo:hi], table_words[1][:].bitcast(U32).indirect(entries(offs_t, lo, hi)))
        h = sb.tile([N, S], F32, name="h")
        copies_out = (nc.scalar.copy, nc.vector.tensor_copy, nc.scalar.copy)
        for bank, (lo, hi), copy_out in zip(banks, BANK_COLS, copies_out):
            nc.tensor.matmul_mx(
                out=bank[:], lhsT=w_codes[:, N : 2 * N].bitcast(FP8X4), lhsT_scale=w_scales[:, N : 2 * N],
                rhs=x_codes1[:, lo:hi].bitcast(FP8X4), rhs_scale=x_planes[:, S + lo : S + hi], start=False, stop=True,
            )
            copy_out(h[:, lo:hi], bank[:])

        space = psum.tile([P, D * V], F32, name="space", tag="bank0")
        for d in range(D):
            for b in range(V // P):
                nc.tensor.transpose(
                    space[:, d * V + b * P : d * V + (b + 1) * P],
                    space_cols[:, b, d : d + 1].to_broadcast([P, P]),
                    identity[:],
                )

        hc = sb.tile([N, V], F32, name="hc")
        h1 = sb.tile([N, HALF_V], F32, name="h1")
        diff = sb.tile([N, D * V], F32, name="diff")
        diff_sq = sb.tile([N, D * V], F32, name="diff_sq")
        alike = sb.tile([N, D * V], F32, name="alike")
        wt = sb.tile([N, D * V], F32, name="wt")
        far = sb.tile([N, D * V], F32, name="far")
        pull = sb.tile([N, D * V], F32, name="pull")
        den = sb.tile([N, V], F32, name="den")
        den_sq = sb.tile([N, V], F32, name="den_sq")
        den_rsqrt = sb.tile([N, V], F32, name="den_rsqrt")
        inv_den = sb.tile([N, V], F32, name="inv_den")
        base = sb.tile([N, V], F32, name="base")
        top = sb.tile([N, V], F32, name="top")
        result = sb.tile([N, V], F32, name="result", align_bytes=256)
        q1, q2 = V // 4, V // 2

        def of(tile, d, lo, hi):
            return tile[:, d * V + lo : d * V + hi]

        def centre_on_scalar(lo, hi):
            nc.scalar.activation(hc[:, lo:hi], h[:].indirect(entries(cen_t, lo, hi)), ACT.Copy)

        def centre_on_vector(lo, hi):
            nc.vector.tensor_copy(hc[:, lo:hi], h[:].indirect(entries(cen_t, lo, hi)))

        def look_up_diff(d, lo, hi):
            nc.vector.tensor_tensor(of(diff, d, lo, hi), h[:].indirect(entries(pos_t[d], lo, hi)), hc[:, lo:hi], ALU.subtract)

        def square_on_scalar(d, lo, hi):
            nc.scalar.activation(of(diff_sq, d, lo, hi), of(diff, d, lo, hi), ACT.Square)

        def square_on_vector(d, lo, hi):
            nc.vector.tensor_tensor(of(diff_sq, d, lo, hi), of(diff, d, lo, hi), of(diff, d, lo, hi), ALU.mult)

        def range_weight(d, lo, hi):
            nc.scalar.activation(of(alike, d, lo, hi), of(diff_sq, d, lo, hi), ACT.Exp, scale=sharp_t[:])

        def make_far(d, lo, hi):
            nc.vector.scalar_tensor_tensor(of(far, d, lo, hi), of(diff, d, lo, hi), -SHARPEN, hc[:, lo:hi], ALU.mult, ALU.add)

        def weight(d, lo, hi):
            nc.vector.tensor_tensor(of(wt, d, lo, hi), of(alike, d, lo, hi), of(space, d, lo, hi), ALU.mult)

        def make_pull(d, lo, hi):
            nc.vector.tensor_tensor(of(pull, d, lo, hi), of(wt, d, lo, hi), of(far, d, lo, hi), ALU.mult)

        def make_den(lo, hi):
            nc.vector.scalar_tensor_tensor(den[:, lo:hi], of(wt, 0, lo, hi), 1.0, of(wt, 1, lo, hi), ALU.add, ALU.add)

        def square_den(lo, hi):
            nc.vector.tensor_tensor(den_sq[:, lo:hi], den[:, lo:hi], den[:, lo:hi], ALU.mult)

        def make_base(lo, hi):
            nc.vector.tensor_tensor(base[:, lo:hi], of(pull, 0, lo, hi), hc[:, lo:hi], ALU.add)

        def make_top(lo, hi):
            nc.vector.tensor_tensor(top[:, lo:hi], base[:, lo:hi], of(pull, 1, lo, hi), ALU.add)

        def invert(lo, hi):
            nc.scalar.activation(inv_den[:, lo:hi], den_sq[:, lo:hi], ACT.Abs_reciprocal_sqrt)

        def root(lo, hi):
            nc.scalar.activation(den_rsqrt[:, lo:hi], den[:, lo:hi], ACT.Abs_reciprocal_sqrt)

        def square_root(lo, hi):
            nc.scalar.activation(inv_den[:, lo:hi], den_rsqrt[:, lo:hi], ACT.Square)

        def finish(lo, hi, queue):
            nc.vector.tensor_tensor(result[:, lo:hi], top[:, lo:hi], inv_den[:, lo:hi], ALU.mult)
            queue.dma_start(out=out[:, lo:hi], in_=result[:, lo:hi])

        centre_on_scalar(q2, V)
        nc.scalar.activation(h1[:], h[:].indirect(entries(pos_t[1], q2, V)), ACT.Copy)
        centre_on_vector(0, q1)
        centre_on_vector(q1, q2)
        look_up_diff(0, 0, q1)
        look_up_diff(0, q1, q2)
        look_up_diff(0, q2, V)
        look_up_diff(1, 0, q2)
        nc.vector.tensor_tensor(of(diff, 1, q2, V), h1[:], hc[:, q2:V], ALU.subtract)
        square_on_scalar(0, 0, q2)
        square_on_scalar(0, q2, V)
        range_weight(0, 0, V)
        square_on_scalar(1, 0, q2)
        range_weight(1, 0, q2)
        make_far(0, 0, V)
        square_on_vector(1, q2, V)
        range_weight(1, q2, V)
        make_far(1, 0, V)
        weight(0, 0, V)
        weight(1, 0, V)
        make_pull(0, 0, V)
        make_den(0, V)
        make_base(0, V)
        make_pull(1, 0, q2)
        square_den(0, q2)
        make_pull(1, q2, V)
        root(q2, V)
        invert(0, q2)
        square_root(q2, V)
        make_top(0, q2)
        make_top(q2, V)
        finish(0, q2, nc.scalar)
        finish(q2, V, nc.scalar)
